import numpy as np, ml_dtypes
CORES = [9,25,41,57]
N = 4
BF = ml_dtypes.bfloat16
def gentries(a):
    return np.ascontiguousarray(a.reshape(8, 16, -1).transpose(0, 2, 1)).reshape(8, -1)
def gtable(e):
    e = np.asarray(e); return np.ascontiguousarray(e.reshape(8, -1, 16).transpose(0, 2, 1)).reshape(128, -1).astype(np.int32)
V, CAP, D, R = 64, 16, 4, 2
def cube():
    P = np.indices((4, 4, 4, 4)).reshape(4, -1).T; P = P[(np.sort(P, 1) == np.arange(4)).all(1)]
    w = np.array([64, 16, 4, 1]); at = np.zeros(256, np.int64); at[P @ w] = np.arange(24)
    return at[P[:, P] @ w]
def cyclic():
    i = np.arange(24); return (i[:, None] + i) % 24
def dihedral():
    i = np.arange(24); r = i % 12; s = i // 12
    return (r[:, None] + np.where(s[:, None] == 1, -r, r)) % 12 + 12 * (s[:, None] ^ s)
def labelled(rng, plain=0, mixed=False):
    res = np.zeros((8, 24, 24), np.int64)
    for g in range(8):
        c = cyclic() if mixed and g in (2, 3) else dihedral() if mixed and g in (4, 5) else cube()
        lab = np.arange(24) if g < plain else rng.permutation(24)
        res[g][lab[:, None], lab[None, :]] = lab[c]
    return res
def values(rng):
    return rng.standard_normal((N, 128, V * 24), dtype=np.float32) * np.exp2(rng.integers(-2, 3, (N, 128, 1))).astype(np.float32)
def raw(rng, plain=0, mixed=False):
    q = (np.arange(N)[:, None, None, None] + 1 + rng.integers(0, N - 1, (N, 8, D, V))) % N
    slot = V + q * CAP + rng.integers(0, CAP, (N, 8, D, V)); own = rng.integers(0, V, (N, 8, D, V))
    return {"x": values(rng), "pose": rng.integers(0, 24, (N, 8, V)), "act": rng.integers(0, 24, (N, 8, R - 1, V)), "c": labelled(rng, plain, mixed),
            "shown": np.argsort(rng.random((N, 8, N, V)), -1)[..., :CAP], "nbr": np.where(rng.random((N, 8, D, V)) < 0.5, own, slot)}
def glists(a):
    return np.stack([gtable(v.reshape(8, -1)) for v in a])
def pack(d):
    c = d["c"]; rel = np.argsort(c, 2).transpose(0, 2, 1)
    every = lambda t: np.repeat(np.ascontiguousarray(t).reshape(1, 8, 576).astype(np.int32), N, 0)
    return {"x": np.ascontiguousarray(d["x"].astype(np.float32)), "pose": glists(d["pose"]), "act": glists(d["act"]), "rel": every(rel), "ct": every(c), "shown": glists(d["shown"]), "nbr": glists(d["nbr"])}
def setup_inputs(rng):
    return pack(raw(rng))
def setup_inputs_full(rng):
    d = raw(rng, mixed=True)
    for r in range(N):
        s = np.concatenate([V + q * CAP + np.arange(CAP) for q in range(N) if q != r])
        for g in range(8):
            flat = d["nbr"][r, g].reshape(-1).copy(); flat[rng.permutation(D * V)[:len(s)]] = s; d["nbr"][r, g] = flat.reshape(D, V)
    return pack(d)
def setup_inputs_repeat(rng):
    d = raw(rng); a, b, e, w = rng.permutation(N)[:4]; n = d["nbr"]
    n[a] = rng.integers(0, V, (8, D, V)); n[a, :, 0] = np.arange(V)
    n[b] = V + a * CAP + rng.integers(0, CAP, (8, D, V))
    n[e] = n[e][:, :1]; q0 = 1 if e == 0 else 0; q1 = N - 2 if e == N - 1 else N - 1
    n[e, :, :, 0] = 0; n[e, :, :, V - 1] = V - 1; n[e, :, :, 1] = V + q1 * CAP + CAP - 1; n[e, :, :, 2] = V + q0 * CAP
    d["shown"][w] = d["shown"][w][..., :1]
    return pack(d)
def setup_inputs_below(rng):
    d = raw(rng); k = rng.integers(0, 87, 8); k[rng.integers(0, 8)] = 86
    d["x"] = -rng.integers(1, 200, (N, 128, V * 24)).astype(np.float32) * np.repeat(np.exp2(k), 16)[:, None].astype(np.float32); return pack(d)
def setup_inputs_alike(rng):
    d = raw(rng, 2, True)
    for g in range(8):
        if g % 2 == 0:
            d["pose"][:, g] = rng.integers(0, 24); d["act"][:, g] = rng.integers(0, 24, (1, R - 1, 1))
        else:
            d["act"][:, g] = np.argmax((d["c"][g] == np.arange(24)).all(1))
    return pack(d)
def setup_inputs_spread(rng):
    d = raw(rng); k = (N, 1, V * 24)
    d["x"] = d["x"] * (np.exp2(rng.integers(-6, 7, k)) * (rng.random(k) > 0.0625)).astype(np.float32); return pack(d)
def check_inputs(d):
    bad = []; j = np.arange(24)
    def within(a, top): return bool((a >= 0).all() and (a < top).all())
    if not np.isfinite(d["x"]).all(): bad.append("finite")
    elif not (np.abs(d["x"]) <= 2.0 ** 94).all(): bad.append("size")
    if not within(d["pose"], 24): bad.append("pose")
    if not within(d["act"], 24): bad.append("act")
    if not within(d["shown"], V): bad.append("shown")
    for r in range(N):
        n = d["nbr"][r]
        if not within(n, V + N * CAP) or ((n >= V + r * CAP) & (n < V + r * CAP + CAP)).any(): bad.append("nbr"); break
    if not (d["rel"] == d["rel"][:1]).all() or not (d["ct"] == d["ct"][:1]).all(): bad.append("tables_alike")
    if not within(d["rel"], 24) or not within(d["ct"], 24): bad.append("tables_range")
    else:
        for g in range(8):
            c = d["ct"][0, g].reshape(24, 24).astype(np.int64); l = d["rel"][0, g].reshape(24, 24).astype(np.int64)
            if not ((np.sort(c, 1) == j).all() and (np.sort(c, 0) == j[:, None]).all() and (c[c] == c[:, c]).all()): bad.append("ct_group"); break
            if not (c[j[None, :], l] == j[:, None]).all(): bad.append("rel"); break
    return bad
def reference(x, pose, act, rel, ct, shown, nbr):
    f = x.reshape(N, 8, 16, V, 24)
    p = np.stack([gentries(v) for v in pose]).astype(np.int64)
    ac = np.stack([gentries(v) for v in act]).reshape(N, 8, R - 1, V).astype(np.int64)
    sh = np.stack([gentries(v) for v in shown]).reshape(N, 8, N, CAP)
    nb = np.stack([gentries(v) for v in nbr]).reshape(N, 8, D, V)
    for t in range(R):
        new = np.zeros(f.shape, np.float32); turned = np.zeros(p.shape, np.int64)
        for r in range(N):
            for g in range(8):
                fe = np.concatenate([f[r, g]] + [f[q, g][:, sh[q, g, r]] for q in range(N)], 1)
                pe = np.concatenate([p[r, g]] + [p[q, g][sh[q, g, r]] for q in range(N)])
                j = nb[r, g]
                e = rel[r, g][p[r, g][None, :] * 24 + pe[j]].astype(np.int64)
                k = ct[r, g][e[:, :, None] * 24 + np.arange(24)]
                new[r, g] = np.maximum.reduce(fe[:, j[:, :, None], k], axis=1)
                if t < R - 1: turned[r, g] = ct[r, g][p[r, g] * 24 + ac[r, g, t]]
        f = new; p = turned
    return {"y": np.ascontiguousarray(f.reshape(N, 128, V * 24))}

@@ -1,0 +1,462 @@
+import numpy as np
+from concourse.bass import DstId, RemoteDMATransfer
+from concourse.mybir import dt, AluOpType, AxisListType, ActivationFunctionType
+
+F, B, I, U = "float32", "bfloat16", "int32", "uint16"
+
+
+def _s(cols, d):
+    return ("sbuf", [128] + (cols if isinstance(cols, list) else [cols]), d)
+
+
+SCRATCH = {
+    "xs": _s(1536, F), "ipo": _s(4, I), "ish": _s(4, I), "iact": _s(4, I), "inbr": _s(16, I), "reln": _s(48, I),
+    "ctn": _s([2, 24], I),
+    "pi": _s(1, I), "ci": _s(4, I), "cf": _s(4, F), "cc": _s(16, F), "pcols": _s(3, F), "bcol": _s(2, F),
+    "cq": _s(128, B), "cqg": _s(128, B), "c48": _s(48, B), "i24": _s(128, F), "c8": _s(96, B), "id124": _s(128, B),
+    "c5": _s(640, B), "sgx": _s([2, 128], B), "w3": _s([2, 128], B), "gm": _s(8, F),
+    "idf": _s(128, F), "sd32": _s(128, F), "su32": _s(128, F),
+    "pu": _s(8, U), "mu": _s(8, U), "shu": _s(4, U), "nbu": _s(16, U),
+    "X": _s(128, F), "xs0": _s(64, F), "xs1": _s(64, F), "cp": _s(48, F), "cfb": _s([4, 16], B), "bd": _s([4, 128], B),
+    "a0s": _s(128, F), "ms": _s(128, F), "cpo": _s(128, F), "ohw": _s(128, B), "ohz": _s(128, B), "oha": _s(128, B),
+    "rd": _s([2, 128], B), "ya": _s(128, B), "ns8": _s(256, B), "ss8": _s(64, B),
+    "ls0": _s(96, U), "l0": _s(96, U), "lr0": _s(384, U), "lr1": _s(128, U), "ls1": _s(24, U),
+    "kb": _s(96, B), "k1": _s(96, B), "k2": _s(96, B), "lf": _s(96, U),
+    "snd0": _s(1152, F), "snd1": _s([3, 384], F), "win0": _s(3072, F), "win1": _s(3072, F),
+    "n1a": _s(768, F), "n1b": _s(768, F), "yo": _s(1536, F),
+}
+for _t in range(2):
+    for _k in range(3):
+        for _n in ("ga", "gb", "ma", "mb"):
+            SCRATCH["%s%d%d" % (_n, _t, _k)] = _s(512, F)
+for _b in range(8):
+    SCRATCH["bank%d" % _b] = ("psum", [128, 8, 64] if _b == 3 else [128, 512], F)
+SEMAPHORES = ["cv", "cs", "cte", "cg", "arr0", "arr1k0", "arr1k1", "arr1k2", "sent"] + ["ld%d" % i for i in range(10)] + ["st%d" % i for i in range(8)]
+AF = ActivationFunctionType
+COPY, IDENT, SIGN = AF.Copy, AF.Identity, AF.Sign
+A = AluOpType
+
+
+def _queues(g, T):
+    q = {"V": g.vector, "S": g.scalar, "T": g.tensor, "G": g, "Y": g.sync}
+    csem = {"V": "cv", "S": "cs", "T": "cte", "G": "cg"}
+    cnt = {}
+    known = {e: {} for e in q}
+    wrote, read = {}, {}
+
+    def after(e, tok):
+        sem, val, snap = tok[1], tok[2], tok[3]
+        if known[e].get(sem, 0) < val:
+            q[e].wait_ge(T.sem[sem], val)
+            known[e][sem] = val
+            for s, v in snap.items():
+                if known[e].get(s, 0) < v:
+                    known[e][s] = v
+
+    def op(e, fn, reads=(), writes=(), sem=None, inc=1, signal=True):
+        toks = []
+        for k in reads:
+            if k in wrote:
+                toks.append(wrote[k])
+            if k.startswith("bank"):
+                toks += [t for t in read.get(k, []) if t[0] != e]
+        for k in writes:
+            if k in wrote and not (e == "T" and wrote[k][0] == "T"):
+                toks.append(wrote[k])
+            toks += [t for t in read.get(k, []) if t[0] != e]
+        best = {}
+        for t in toks:
+            if t[1] not in best or best[t[1]][2] < t[2]:
+                best[t[1]] = t
+        for t in best.values():
+            after(e, t)
+        ins = fn()
+        if not signal:
+            return
+        name = sem or csem[e]
+        cnt[name] = cnt.get(name, 0) + inc
+        ins.then_inc(T.sem[name], inc)
+        tok = (e, name, cnt[name], dict(known[e]))
+        for k in reads:
+            read.setdefault(k, []).append(tok)
+        for k in writes:
+            wrote[k] = tok
+            read[k] = []
+
+    def wait(e, sem, val):
+        if known[e].get(sem, 0) < val:
+            q[e].wait_ge(T.sem[sem], val)
+            known[e][sem] = val
+    return q, op, wait, cnt
+
+
+def rank_program(g, core, T, topo):
+    r = T.rank_of(core)
+    if r is None:
+        return
+    ranks = list(T.cores)
+    n_ranks = len(ranks)
+    dests = [(r + 1 + j) % n_ranks for j in range(n_ranks - 1)]
+    q, op, wait, cnt = _queues(g, T)
+    v, s, te = g.vector, g.scalar, g.tensor
+
+    def share(a, b, i):
+        es = topo.engines(a, b)
+        h = len(es) // 2
+        return (es[:h], es[h:], es)[i]
+    nout = sum(len(share(core, ranks[d], j)) for j, d in enumerate(dests))
+    nin = sum(len(share(ranks[(r - 1 - j) % n_ranks], core, j)) for j in range(n_ranks - 1))
+
+    def bank(b):
+        return T["bank%d" % b]
+
+    def ts(out, in0, s1, s2, o0, o1, reads, writes):
+        if o1 is None:
+            op("V", lambda: v.tensor_scalar(out, in0, s1, None, o0), reads, writes)
+        else:
+            op("V", lambda: v.tensor_scalar(out, in0, s1, s2, o0, o1), reads, writes)
+
+    def tt(out, a, b, o, reads, writes):
+        op("V", lambda: v.tensor_tensor(out, a, b, o), reads, writes)
+
+    def vcopy(out, a, reads, writes):
+        op("V", lambda: v.tensor_copy(out, a), reads, writes)
+
+    def act(out, a, reads, writes, scale=None, bias=None):
+        if bias is not None:
+            op("S", lambda: s.activation(out, a, IDENT, bias=bias), reads, writes)
+        elif scale is None:
+            op("S", lambda: s.activation(out, a, COPY), reads, writes)
+        else:
+            op("S", lambda: s.activation(out, a, COPY, scale=scale), reads, writes)
+
+    def mmo(b, out, parts, first=True, last=True):
+        for i, (l, rh, keys) in enumerate(parts):
+            op("T", lambda: te.matmul(out, l, rh, first and i == 0, last and i == len(parts) - 1), keys, ["bank%d" % b])
+
+    def mm(b, c0, n, parts, first=True, last=True):
+        mmo(b, bank(b)[:, c0:c0 + n], parts, first, last)
+
+    op("Y", lambda: g.sync.dma_start(T.reln[:, 0:24], T.rel[:, 0:384]), [], ["relA"], "ld0", 16)
+    op("S", lambda: s.dma_start(T.ipo[:], T.pose[:]), [], ["ipo"], "ld1", 16)
+    op("Y", lambda: g.sync.dma_start(T.reln[:, 24:48], T.rel[:, 192:576]), [], ["relB"], "ld2", 16)
+    op("S", lambda: s.dma_start(T.ish[:], T.shown[:]), [], ["ish"], "ld3", 16)
+    op("Y", lambda: g.sync.dma_start(T.xs[:], T.x[:]), [], ["xs"], "ld4", 16)
+    op("Y", lambda: g.sync.dma_start(T.iact[:], T.act[:]), [], ["iact"], "ld5", 16)
+    for y in range(2):
+        op("Y", lambda: g.sync.dma_start(T.ctn[:, y, :], T.ct[:, 192 * y:192 * y + 384]), [], ["ctn%d" % y], "ld%d" % (6 + y), 16)
+    op("Y", lambda: g.sync.dma_start(T.inbr[:], T.nbr[:]), [], ["inbr"], "ld8", 16)
+    relk, ctk = ["relA", "relB"], ["ctn0", "ctn1"]
+
+    def iota(out, pat, base, cm, key, flag=True):
+        if flag:
+            op("G", lambda: g.iota(out, pat, base, cm, allow_small_or_imprecise_dtypes=True), [], [key])
+        else:
+            op("G", lambda: g.iota(out, pat, base, cm), [], [key])
+    iota(T.pi[:], [[1, 1]], 0, 1, "pi", False)
+    iota(T.pcols[:], [[8, 3]], -8, 1, "pcols")
+    iota(T.cq[:], [[1, 128]], 0, 0, "cq")
+    iota(T.i24[:], [[0, 2], [24, 64]], 0, 0, "i24")
+    iota(T.c48[:], [[0, 2], [1, 24]], 0, 0, "c48")
+    iota(T.cqg[:], [[1, 8], [0, 16]], 0, 0, "cqg")
+    op("V", lambda: v.tensor_scalar(T.ci[:, 0:1], T.pi[:], 4, None, A.arith_shift_right), ["pi"], ["ci0"])
+    op("V", lambda: v.tensor_scalar(T.ci[:, 1:2], T.pi[:], 15, None, A.bitwise_and), ["pi"], ["ci1"])
+    op("V", lambda: v.tensor_scalar(T.ci[:, 2:3], T.pi[:], 3, 1, A.arith_shift_right, A.bitwise_and), ["pi"], ["ci2"])
+    op("V", lambda: v.tensor_scalar(T.ci[:, 3:4], T.pi[:], 7, None, A.bitwise_and), ["pi"], ["ci3"])
+    vcopy(T.cf[:], T.ci[:], ["ci0", "ci1", "ci2", "ci3"], ["cf"])
+    gc, pc, hc, k8 = (T.cf[:, j:j + 1] for j in range(4))
+    ccn = {}
+
+    def col(name):
+        return T.cc[:, ccn[name]:ccn[name] + 1]
+
+    def mkcol(name, src, m, a):
+        ccn[name] = len(ccn)
+        op("S", lambda: s.activation(col(name), src, COPY, bias=float(a), scale=float(m)), ["cf"], ["c_" + name])
+    mkcol("nh", hc, -1, 1)
+    mkcol("p8", pc, 1, 8)
+    mkcol("big", hc, -100, 100)
+    mkcol("h8", hc, 8, -4)
+    colPm8, colP, colPp8 = (T.pcols[:, j:j + 1] for j in range(3))
+
+    def tile(o1, src, s1, key, reads, s2=None):
+        ts(o1, T[src][:], s1, s2, A.is_equal, A.mult if s2 is not None else None, [src] + reads, [key])
+    down, same, up, low, high = (T.c5[:, 128 * j:128 * j + 128] for j in range(5))
+    tile(down, "cq", colPm8, "down", ["pcols", "cf"], hc)
+    tile(same, "cq", colP, "same", ["pcols"])
+    tile(up, "cq", colPp8, "up", ["pcols", "c_nh"], col("nh"))
+    act(T.sd32[:], down, ["down"], ["sd32"])
+    act(T.idf[:], same, ["same"], ["idf"])
+    act(T.su32[:], up, ["up"], ["su32"])
+
+    vcopy(T.pu[:, 0:4], T.ipo[:], ["ipo"], ["pua"])
+    ts(T.pu[:, 4:8], T.ipo[:], 24.0, None, A.add, None, ["ipo"], ["pub"])
+    vcopy(T.shu[:], T.ish[:], ["ish"], ["shu"])
+    puk = ["pua", "pub"]
+    tt(T.X[:], T.reln[:].indirect(T.pu[:]), T.i24[:], A.add, relk + puk + ["i24"], ["X"])
+    vcopy(T.xs0[:], T.X[:, 0:64].indirect(T.shu[:]), ["X", "shu"], ["xs0"])
+    act(T.xs1[:], T.X[:, 64:128].indirect(T.shu[:]), ["X", "shu"], ["xs1"])
+    act(T.a0s[:], T.c48[:].indirect(T.pu[:]), puk + ["c48"], ["a0s"])
+
+    def middle(b, out, d, u):
+        mmo(b, out, [d, u])
+    middle(0, bank(0)[:, 0:32], (T.sd32[:], T.xs1[:, 0::2], ["sd32", "xs1"]), (T.su32[:], T.xs0[:, 1::2], ["su32", "xs0"]))
+    mmo(1, bank(1)[:, 0:96:3], [(T.idf[:], T.X[:, 0:64:2], ["idf", "X"])])
+    middle(1, bank(1)[:, 1:96:3], (T.sd32[:], T.X[:, 64:128:2], ["sd32", "X"]), (T.su32[:], T.X[:, 1:64:2], ["su32", "X"]))
+    mmo(1, bank(1)[:, 2:96:3], [(T.idf[:], T.X[:, 65:128:2], ["idf", "X"])])
+    vcopy(T.ls0[:, 0::3], T.xs0[:, 0::2], ["xs0"], ["ls00"])
+    vcopy(T.ls0[:, 2::3], T.xs1[:, 1::2], ["xs1"], ["ls02"])
+    tile(low, "cq", colP, "low", ["pcols", "c_nh"], col("nh"))
+    tile(high, "cq", colP, "high", ["pcols", "cf"], hc)
+    ts(T.gm[:], T.cq[:, 0:8], gc, None, A.is_equal, None, ["cq", "cf"], ["gm"])
+    vcopy(T.ls0[:, 1::3], bank(0)[:, 0:32], ["bank0"], ["ls01"])
+    lsk = ["ls00", "ls01", "ls02", "xs"]
+    l0k = ["l0", "xs"]
+
+    def slot0(e, j, a, b, key):
+        c = 24 * dests[j]
+        src, out = T.xs[:].indirect(T.ls0[:, c + a:c + b]), T.snd0[:, 384 * j + 16 * a:384 * j + 16 * b]
+        if e == "V":
+            vcopy(out, src, lsk, [key])
+        else:
+            act(out, src, lsk, [key])
+    slot0("V", 0, 0, 12, "snd0a")
+    slot0("S", 0, 12, 24, "snd0b")
+    slot0("V", 1, 0, 24, "snd0c")
+    slot0("S", 2, 0, 24, "snd0d")
+
+    def send(out, srcs, sem, keys, pair):
+        at = [topo.addr(ranks[d])[:2] for d in dests]
+
+        def mask(j, i):
+            return sum(1 << e for e in share(core, ranks[dests[j]], i))
+        alone = 3 - sum(pair)
+        two = [RemoteDMATransfer(dst_ids=[DstId(rid=at[j][0], pnc=at[j][1])], dma_engine_mask=mask(j, i), remote_sem=T.sem[sem], srcs=[srcs[j]], dsts=[out], alu_op=0) for i, j in enumerate(pair)]
+
+        def fused():
+            op("G", lambda: g.remote_dma_fused(two, local_sem=T.sem.sent), keys[pair[0]] + keys[pair[1]], [], signal=False)
+
+        def single():
+            op("G", lambda: g.remote_dma(out, srcs[alone], T.sem[sem], T.sem.sent, at[alone][1], at[alone][0], mask(alone, 2)), keys[alone], [], signal=False)
+        for f in ((single, fused) if alone == 0 else (fused, single)):
+            f()
+    c0 = 24 * (64 + 16 * r)
+    send(T.win0[:, c0:c0 + 384], [T.snd0[:, 384 * j:384 * j + 384] for j in range(3)], "arr0", [["snd0a", "snd0b"], ["snd0c"], ["snd0d"]], (1, 2))
+    iota(T.bcol[:], [[-16, 2]], -15, 0, "bcol")
+    iota(T.c8[:], [[0, 2], [16, 16], [4, 3]], 248, 0, "c8a")
+
+    def own(e, a, b, key):
+        src, out = T.xs[:].indirect(T.l0[:, a:b]), T.win0[:, 16 * a:16 * b]
+        if e == "V":
+            vcopy(out, src, l0k, [key])
+        else:
+            act(out, src, l0k, [key])
+    vcopy(T.l0[:], bank(1)[:, 0:96], ["bank1"], ["l0"])
+    tile(T.sgx[:, 0, :], "cqg", gc, "sgx0", ["cf"], pc)
+    tile(T.sgx[:, 1, :], "cqg", gc, "sgx1", ["cf", "c_p8"], col("p8"))
+    act(T.w3[:, 0, :], low, ["low"], ["w3l"], 3.0)
+    act(T.w3[:, 1, :], high, ["high"], ["w3h"], 3.0)
+    own("V", 0, 8, "win0a")
+    own("S", 72, 96, "win0b")
+    vcopy(T.mu[:, 0:4], T.iact[:], ["iact"], ["mua"])
+    ts(T.mu[:, 4:8], T.iact[:], 24.0, None, A.add, None, ["iact"], ["mub"])
+    vcopy(T.cp[:, 0:24], T.ctn[:, 0, :], ["ctn0"], ["cpa"])
+    ts(T.cp[:, 24:48], T.ctn[:, 1, :], col("big"), None, A.add, None, ["ctn1", "c_big"], ["cpb"])
+    muk, cpk = ["mua", "mub"], ["cpa", "cpb"]
+    tt(T.ohw[:], T.cp[:].indirect(T.mu[:]), T.a0s[:], A.is_equal, cpk + muk + ["a0s"], ["ohw"])
+    act(T.cpo[:], T.cp[:].indirect(T.pu[:]), cpk + puk, ["cpo"])
+    for y in range(2):
+        vcopy(T.cfb[:, y::2, :], T.ctn[:, :, 8 * y:8 * y + 16], ctk, ["cf%d" % y])
+    vcopy(T.nbu[:], T.inbr[:], ["inbr"], ["nbu"])
+    for c in range(2):
+        mm(2, 64 * c, 64, [(T.sgx[:, x, :], T.ohw[:, 64 * x:64 * x + 64], ["sgx%d" % x, "ohw"]) for x in range(2)])
+    for j in range(8):
+        out, sc = T.bd[:, :, 16 * j:16 * j + 16], T.gm[:, j:j + 1]
+        if j % 2:
+            ts(out, T.cfb[:], sc, None, A.mult, None, ["cf0", "cf1", "gm"], ["bd%d" % j])
+        else:
+            act(out, T.cfb[:], ["cf0", "cf1", "gm"], ["bd%d" % j], sc)
+    bdk = ["bd%d" % j for j in range(8)]
+    tt(T.ohz[:], T.cpo[:], bank(2)[:, 0:128], A.is_equal, ["cpo", "bank2"], ["ohz"])
+    own("V", 8, 40, "win0c")
+
+    def rows(b, oh, key):
+        for y in range(2):
+            out = bank(b)[:, y, :] if b == 3 else bank(b)[:, 64 * y:64 * y + 64]
+            mmo(b, out, [(T.bd[:, 2 * x + y, :], oh[:, 64 * x:64 * x + 64], bdk + [key]) for x in range(2)])
+    rows(3, T.ohz, "ohz")
+    act(T.ns8[:], T.cq[:].indirect(T.nbu[:]), ["cq", "nbu"], ["ns8"], 8.0)
+    for n in range(2):
+        act(T.rd[:, :, 64 * n:64 * n + 64], T.bank3[:, 0:2, :], ["bank3"], ["rd%d" % n])
+    rdk = ["rd%d" % n for n in range(2)]
+    own("S", 60, 72, "win0d")
+    act(T.ms[:, 0:64], T.c48[:].indirect(T.mu[:, 0:4]), ["c48", "mua"], ["ms0"])
+    act(T.ms[:, 64:128], T.c48[:].indirect(T.mu[:, 4:8]), ["c48", "mub", "c_big"], ["ms1"], bias=col("big"))
+    ev, od = T.ns8[:, 0::2], T.ns8[:, 1::2]
+    r1e, r1o, r2e, r2o = (T.rd[:, e, o::2] for e in range(2) for o in range(2))
+    turn = [((low, r1e, "low"), (up, r1o, "up")), ((low, r2e, "low"), (high, r1o, "high")), ((down, r2e, "down"), (high, r2o, "high"))]
+    for k in range(3):
+        mm(4 + k, 0, 128, [(T.w3[:, 0, :], ev, ["w3l", "ns8"])], last=False)
+        for n in range(2):
+            mm(4 + k, 64 * n, 64, [(t, rh, [key] + rdk) for t, rh, key in turn[k]], first=False, last=False)
+        mm(4 + k, 0, 128, [(T.w3[:, 1, :], od, ["w3h", "ns8"])], first=False)
+    own("V", 40, 60, "win0e")
+    act(T.id124[:], same, ["same"], ["id124"], 124.0)
+    act(T.c8[:, 1::3], T.c8[:, 1::3], ["c8a", "c_h8"], ["c8b"], bias=col("h8"))
+    act(T.ss8[:], T.cq[:].indirect(T.shu[:]), ["cq", "shu"], ["ss8"], 8.0)
+    mm(7, 0, 128, [(low, ev, ["low", "ns8"]), (high, od, ["high", "ns8"])])
+    for j, d in enumerate(dests):
+        mm(7, 128 + 8 * j, 8, [(low, T.ss8[:, 16 * d:16 * d + 16:2], ["low", "ss8"]), (high, T.ss8[:, 16 * d + 1:16 * d + 16:2], ["high", "ss8"])])
+    for k in range(3):
+        vcopy(T.lr0[:, 128 * k:128 * k + 128], bank(4 + k)[:, 0:128], ["bank%d" % (4 + k)], ["lr0%d" % k])
+        if k == 0:
+            tt(T.oha[:], T.reln[:].indirect(T.pu[:]), T.ms[:], A.is_equal, relk + puk + ["ms0", "ms1"], ["oha"])
+            rows(2, T.oha, "oha")
+
+    def last1():
+        act(T.ya[:], bank(2)[:, 0:128], ["bank2"], ["ya"])
+        mmo(5, bank(5)[:, 0:96:3], [(same, T.ya[:, 0:64:2], ["same", "ya"])])
+        middle(5, bank(5)[:, 1:96:3], (down, T.ya[:, 64:128:2], ["down", "ya"]), (up, T.ya[:, 1:64:2], ["up", "ya"]))
+        mmo(5, bank(5)[:, 2:96:3], [(same, T.ya[:, 65:128:2], ["same", "ya"])])
+
+    def last2():
+        act(T.kb[:], bank(5)[:, 0:96], ["bank5"], ["kb"])
+        for j in range(2):
+            out, b, key = T["k%d" % (j + 1)], T.bcol[:, j:j + 1], "k%d" % (j + 1)
+            op("S", lambda: s.activation(out[:], bank(5)[:, 0:96], SIGN, bias=b, scale=2.0), ["bank5", "bcol"], [key])
+        mm(6, 0, 96, [(same, T.c8[:], ["same", "c8a", "c8b"]), (same, T.kb[:], ["kb"])] + [(T.id124[:], T[k][:], ["id124", k]) for k in ("k1", "k2")])
+
+    hs = [slice(256 * h, 256 * h + 256) for h in range(2)]
+    pb = {(0, 0): 0, (0, 1): 1, (0, 2): 2, (1, 0): 4, (1, 1): 5, (1, 2): 6}
+    pcopy = {(1, 0, 0): 7, (1, 1, 0): 0}
+
+    def win(t, k):
+        return T.win0[:] if t == 0 else T.win1[:, 1024 * k:1024 * k + 1024]
+
+    def lst(t, k, n, a=0, b=32):
+        c = 128 * k + 32 * n if t == 0 else 32 * n
+        return T.lr0[:, c + a:c + b] if t == 0 else T.lr1[:, c + a:c + b]
+
+    def keys(t, k):
+        return ["win0a", "win0b", "win0c", "win0d", "win0e", "lr0%d" % k] if t == 0 else ["f1%d0" % k, "f1%d1" % k, "lr1"]
+
+    def arrived(e, t, k):
+        wait(e, "arr0" if t == 0 else "arr1k%d" % k, nin)
+
+    def buf(n, t, k):
+        return T["%s%d%d" % (n, t, k)]
+
+    def bk(n, t, k, h):
+        return "%s%d%dh%d" % (n, t, k, h)
+
+    def first(e, t, k, h):
+        arrived(e, t, k)
+        out, src, ky = buf("ga", t, k)[:, hs[h]], win(t, k).indirect(lst(t, k, 0, 16 * h, 16 * h + 16)), keys(t, k)
+        if e == "V":
+            vcopy(out, src, ky, [bk("ga", t, k, h)])
+        else:
+            act(out, src, ky, [bk("ga", t, k, h)])
+
+    def gather(t, k, n, halves=(0, 1)):
+        arrived("S", t, k)
+        nm = "g" + "ab"[n]
+        whole = t == 0 and k > 0
+        if whole:
+            act(buf(nm, t, k)[:], win(t, k).indirect(lst(t, k, n)), keys(t, k), [bk(nm, t, k, 0), bk(nm, t, k, 1)])
+        for h in halves:
+            if not whole:
+                act(buf(nm, t, k)[:, hs[h]], win(t, k).indirect(lst(t, k, n, 16 * h, 16 * h + 16)), keys(t, k), [bk(nm, t, k, h)])
+            if n == 1 and (t, k, h) in pcopy:
+                b = pcopy[t, k, h]
+                act(bank(b)[:, hs[h]], buf(nm, t, k)[:, hs[h]], [bk(nm, t, k, h)], ["bank%d" % b])
+            elif n == 1:
+                mm(pb[t, k], 256 * h, 256, [(T.idf[:], buf(nm, t, k)[:, hs[h]], ["idf", bk(nm, t, k, h)])])
+
+    def result(t, k, h):
+        if t == 0:
+            return T.win1[:, 1024 * k + 256 * h:1024 * k + 256 * h + 256], "f1%d%d" % (k, h)
+        return T["n1" + "ab"[h]][:, 256 * k:256 * k + 256], "n1%d%d" % (h, k)
+
+    def part(t, k, n, h):
+        arrived("V", t, k)
+        src, dst = {2: ("ga", "ma"), 3: ("ma", "mb"), 1: ("mb", "")}[n]
+        out, key = result(t, k, h) if n == 1 else (buf(dst, t, k)[:, hs[h]], bk(dst, t, k, h))
+        tt(out, win(t, k).indirect(lst(t, k, n, 16 * h, 16 * h + 16)), buf(src, t, k)[:, hs[h]], A.max, keys(t, k) + [bk(src, t, k, h)], [key])
+
+    def join(t, k, h):
+        out, key = result(t, k, h)
+        b = pcopy.get((t, k, h), pb[t, k])
+        tt(out, bank(b)[:, hs[h]], buf("mb", t, k)[:, hs[h]], A.max, ["bank%d" % b, bk("mb", t, k, h)], [key])
+
+    both, one = (0, 1), (1,)
+    moved = {(0, 0): one, (0, 1): both, (0, 2): both, (1, 0): (1, 0), (1, 1): (1, 0), (1, 2): one}
+
+    def vector(t, order):
+        for k, n, h in order:
+            if n == 1 and h in moved[t, k]:
+                join(t, k, h)
+            else:
+                part(t, k, n, h)
+
+    def block(k):
+        return [(k, n, h) for n in (2, 3, 1) for h in range(2)]
+
+    def slots1(k):
+        w, ky = T.win1[:, 1024 * k:1024 * k + 512], ["f1%d0" % k, "f1%d1" % k, "ls1"]
+        if k < 2:
+            act(T.snd1[:, k, :], w.indirect(T.ls1[:]), ky, ["snd1%d" % k])
+            kk = [["snd1%d" % k]] * 3
+        else:
+            act(T.snd1[:, k, 0:128], w.indirect(T.ls1[:, 0:8]), ky, ["snd12a"])
+            for j, key in ((1, "snd12b"), (2, "snd12c")):
+                vcopy(T.snd1[:, k, 128 * j:128 * j + 128], w.indirect(T.ls1[:, 8 * j:8 * j + 8]), ky, [key])
+            kk = [["snd12a"], ["snd12b"], ["snd12c"]]
+        c0 = 1024 * k + 8 * (64 + 16 * r)
+        send(T.win1[:, c0:c0 + 128], [T.snd1[:, k, 128 * j:128 * j + 128] for j in range(3)], "arr1k%d" % k, kk, (0, 1))
+
+    first("S", 0, 0, 0)
+    first("V", 0, 0, 1)
+    ts(T.lr1[:], bank(7)[:, 0:128], k8, None, A.add, None, ["bank7", "cf"], ["lr1"])
+    ts(T.ls1[:], bank(7)[:, 128:152], k8, None, A.add, None, ["bank7", "cf"], ["ls1"])
+    gather(0, 0, 1, moved[0, 0])
+    gather(0, 1, 1, moved[0, 1])
+    last1()
+    gather(0, 1, 0)
+    gather(0, 2, 1, moved[0, 2])
+    vector(0, block(0))
+    slots1(0)
+    gather(0, 2, 0)
+    vector(0, block(1))
+    slots1(1)
+    last2()
+    vector(0, block(2))
+    slots1(2)
+    vcopy(T.lf[:], bank(6)[:, 0:96], ["bank6"], ["lf"])
+    first("V", 1, 0, 1)
+    first("S", 1, 0, 0)
+    gather(1, 0, 1, moved[1, 0])
+    for k in range(1, 3):
+        gather(1, k, 0)
+        gather(1, k, 1, moved[1, k])
+    vector(1, block(0))
+    vector(1, [(1, 2, 0), (1, 2, 1), (1, 3, 0), (1, 3, 1), (1, 1, 0), (2, 2, 0), (1, 1, 1), (2, 3, 0), (2, 1, 0), (2, 2, 1), (2, 3, 1), (2, 1, 1)])
+
+    nst = [0]
+
+    def final(e, a, b):
+        h = 0 if b <= 48 else 1
+        out, src = T.yo[:, 16 * a:16 * b], T["n1" + "ab"[h]][:].indirect(T.lf[:, a:b])
+        ky = ["lf"] + ["n1%d%d" % (h, k) for k in range(3)]
+        if e == "V":
+            vcopy(out, src, ky, ["yo%d" % a])
+        else:
+            act(out, src, ky, ["yo%d" % a])
+        op("Y", lambda: g.sync.dma_start(T.y[:, 16 * a:16 * b], T.yo[:, 16 * a:16 * b]), ["yo%d" % a], [], "st%d" % nst[0], 16)
+        nst[0] += 1
+    final("S", 0, 24)
+    final("S", 24, 48)
+    final("V", 48, 72)
+    final("S", 72, 96)
+    for name in sorted(cnt):
+        wait("Y", name, cnt[name])
+    wait("G", "sent", (1 + 3) * nout)

@@ -3,6 +3,7 @@ from concourse.bass import DstId, RemoteDMATransfer
 from concourse.mybir import dt, AluOpType, AxisListType, ActivationFunctionType
 
 F, B, I, U = "float32", "bfloat16", "int32", "uint16"
+RW = 160
 
 
 def _s(cols, d):
@@ -13,7 +14,7 @@ SCRATCH = {
     "xs": _s(1536, F), "ipo": _s(4, I), "ish": _s(4, I), "iact": _s(4, I), "inbr": _s(16, I), "reln": _s(48, I),
     "ctn": _s([2, 24], I),
     "pi": _s(1, I), "ci": _s(4, I), "cf": _s(4, F), "cc": _s(16, F), "pcols": _s(3, F), "bcol": _s(2, F),
-    "cq": _s(128, B), "cqg": _s(128, B), "c48": _s(48, B), "i24": _s(128, F), "c8": _s(96, B), "id124": _s(128, B),
+    "cq": _s(128, B), "cqg": _s(128, B), "c48": _s(48, B), "i24": _s(128, F), "c8": _s(96, B), "id60": _s(128, B),
     "c5": _s(640, B), "sgx": _s([2, 128], B), "w3": _s([2, 128], B), "gm": _s(8, F),
     "idf": _s(128, F), "sd32": _s(128, F), "su32": _s(128, F),
     "pu": _s(8, U), "mu": _s(8, U), "shu": _s(4, U), "nbu": _s(16, U),
@@ -23,7 +24,8 @@ SCRATCH = {
     "ls0": _s(96, U), "l0": _s(96, U), "lr0": _s(384, U), "lr1": _s(128, U), "ls1": _s(24, U),
     "kb": _s(96, B), "k1": _s(96, B), "k2": _s(96, B), "lf": _s(96, U),
     "snd0": _s(1152, F), "snd1": _s([3, 384], F), "win0": _s(3072, F), "win1": _s(3072, F),
-    "n1a": _s(768, F), "n1b": _s(768, F), "yo": _s(1536, F),
+    "n1q0": _s(384, F), "n1q1": _s(384, F), "n1q2": _s(384, F), "n1q3": _s(384, F), "yo": _s(1536, F),
+    "hop0": _s(RW, F), "hop1": _s(128, F), "hop2": _s(128, F),
 }
 for _t in range(2):
     for _k in range(3):
@@ -31,7 +33,7 @@ for _t in range(2):
             SCRATCH["%s%d%d" % (_n, _t, _k)] = _s(512, F)
 for _b in range(8):
     SCRATCH["bank%d" % _b] = ("psum", [128, 8, 64] if _b == 3 else [128, 512], F)
-SEMAPHORES = ["cv", "cs", "cte", "cg", "arr0", "arr1k0", "arr1k1", "arr1k2", "sent"] + ["ld%d" % i for i in range(10)] + ["st%d" % i for i in range(8)]
+SEMAPHORES = ["cv", "cs", "cte", "cg", "arr0", "arr1k0", "arr1k1", "arr1k2", "sent", "hop0", "hop1", "hop2"] + ["ld%d" % i for i in range(10)] + ["st%d" % i for i in range(8)]
 AF = ActivationFunctionType
 COPY, IDENT, SIGN = AF.Copy, AF.Identity, AF.Sign
 A = AluOpType
@@ -90,22 +92,59 @@ def _queues(g, T):
     return q, op, wait, cnt
 
 
+def _mask(es):
+    return sum(1 << e for e in es)
+
+
+def _helper(topo, ranks, r):
+    c = ranks[r]
+    return [h for h in topo.cores_of(c) if topo.die(h) != topo.die(c) and h not in ranks
+            and all(topo.may_write(h, d) for d in ranks if d != c)][0]
+
+
+def _inner(topo, ranks, r):
+    out = topo.engines(ranks[r], ranks[(r - 1) % len(ranks)])
+    return [e for e in topo.engines(ranks[r], _helper(topo, ranks, r)) if e not in out]
+
+
+def _hand_on(g, core, T, topo, ranks, r):
+    d = ranks[(r - 1) % len(ranks)]
+    rid, pid = topo.addr(d)[:2]
+    n = len(_inner(topo, ranks, r))
+    c0 = 24 * (64 + 16 * r) + 384 - RW
+    outs = [(T.win0[:, c0:c0 + RW], "arr0")]
+    for k in range(2):
+        c1 = 1024 * k + 8 * (64 + 16 * r)
+        outs.append((T.win1[:, c1:c1 + 128], "arr1k%d" % k))
+    for j, (out, sem) in enumerate(outs):
+        g.wait_ge(T.sem["hop%d" % j], n)
+        g.remote_dma(out, T["hop%d" % j][:], T.sem[sem], T.sem.sent, pid, rid, topo.mask(core, d))
+    g.wait_ge(T.sem.sent, len(outs) * len(topo.engines(core, d)))
+
+
 def rank_program(g, core, T, topo):
     r = T.rank_of(core)
-    if r is None:
-        return
     ranks = list(T.cores)
     n_ranks = len(ranks)
+    if r is None:
+        for rr in range(n_ranks):
+            if _helper(topo, ranks, rr) == core:
+                _hand_on(g, core, T, topo, ranks, rr)
+        return
     dests = [(r + 1 + j) % n_ranks for j in range(n_ranks - 1)]
     q, op, wait, cnt = _queues(g, T)
     v, s, te = g.vector, g.scalar, g.tensor
+    helper, inner = _helper(topo, ranks, r), _inner(topo, ranks, r)
 
     def share(a, b, i):
         es = topo.engines(a, b)
         h = len(es) // 2
         return (es[:h], es[h:], es)[i]
-    nout = sum(len(share(core, ranks[d], j)) for j, d in enumerate(dests))
-    nin = sum(len(share(ranks[(r - 1 - j) % n_ranks], core, j)) for j in range(n_ranks - 1))
+    nout = [len(share(core, ranks[d], j)) for j, d in enumerate(dests)]
+    nin = [len(share(ranks[(r - 1 - j) % n_ranks], core, j)) for j in range(n_ranks - 1)]
+    nrel = len(topo.engines(_helper(topo, ranks, (r + 1) % n_ranks), core))
+    narr = {"arr0": sum(nin) + nrel, "arr1k0": nin[0] + nin[1] + nrel, "arr1k1": nin[0] + nin[1] + nrel, "arr1k2": sum(nin)}
+    nsent = [0]
 
     def bank(b):
         return T["bank%d" % b]
@@ -159,6 +198,8 @@ def rank_program(g, core, T, topo):
     iota(T.i24[:], [[0, 2], [24, 64]], 0, 0, "i24")
     iota(T.c48[:], [[0, 2], [1, 24]], 0, 0, "c48")
     iota(T.cqg[:], [[1, 8], [0, 16]], 0, 0, "cqg")
+    iota(T.bcol[:], [[-16, 2]], -15, 0, "bcol")
+    iota(T.c8[:], [[0, 4], [16, 8], [4, 3]], 120, 0, "c8a")
     op("V", lambda: v.tensor_scalar(T.ci[:, 0:1], T.pi[:], 4, None, A.arith_shift_right), ["pi"], ["ci0"])
     op("V", lambda: v.tensor_scalar(T.ci[:, 1:2], T.pi[:], 15, None, A.bitwise_and), ["pi"], ["ci1"])
     op("V", lambda: v.tensor_scalar(T.ci[:, 2:3], T.pi[:], 3, 1, A.arith_shift_right, A.bitwise_and), ["pi"], ["ci2"])
@@ -194,6 +235,8 @@ def rank_program(g, core, T, topo):
     vcopy(T.shu[:], T.ish[:], ["ish"], ["shu"])
     puk = ["pua", "pub"]
     tt(T.X[:], T.reln[:].indirect(T.pu[:]), T.i24[:], A.add, relk + puk + ["i24"], ["X"])
+    tile(low, "cq", colP, "low", ["pcols", "c_nh"], col("nh"))
+    tile(high, "cq", colP, "high", ["pcols", "cf"], hc)
     vcopy(T.xs0[:], T.X[:, 0:64].indirect(T.shu[:]), ["X", "shu"], ["xs0"])
     act(T.xs1[:], T.X[:, 64:128].indirect(T.shu[:]), ["X", "shu"], ["xs1"])
     act(T.a0s[:], T.c48[:].indirect(T.pu[:]), puk + ["c48"], ["a0s"])
@@ -204,11 +247,14 @@ def rank_program(g, core, T, topo):
     mmo(1, bank(1)[:, 0:96:3], [(T.idf[:], T.X[:, 0:64:2], ["idf", "X"])])
     middle(1, bank(1)[:, 1:96:3], (T.sd32[:], T.X[:, 64:128:2], ["sd32", "X"]), (T.su32[:], T.X[:, 1:64:2], ["su32", "X"]))
     mmo(1, bank(1)[:, 2:96:3], [(T.idf[:], T.X[:, 65:128:2], ["idf", "X"])])
+    ts(T.gm[:], T.cq[:, 0:8], gc, None, A.is_equal, None, ["cq", "cf"], ["gm"])
     vcopy(T.ls0[:, 0::3], T.xs0[:, 0::2], ["xs0"], ["ls00"])
     vcopy(T.ls0[:, 2::3], T.xs1[:, 1::2], ["xs1"], ["ls02"])
-    tile(low, "cq", colP, "low", ["pcols", "c_nh"], col("nh"))
-    tile(high, "cq", colP, "high", ["pcols", "cf"], hc)
-    ts(T.gm[:], T.cq[:, 0:8], gc, None, A.is_equal, None, ["cq", "cf"], ["gm"])
+    tile(T.sgx[:, 0, :], "cqg", gc, "sgx0", ["cf"], pc)
+    tile(T.sgx[:, 1, :], "cqg", gc, "sgx1", ["cf", "c_p8"], col("p8"))
+    act(T.w3[:, 0, :], low, ["low"], ["w3l"], 3.0)
+    act(T.w3[:, 1, :], high, ["high"], ["w3h"], 3.0)
+    act(T.ss8[:], T.cq[:].indirect(T.shu[:]), ["cq", "shu"], ["ss8"], 8.0)
     vcopy(T.ls0[:, 1::3], bank(0)[:, 0:32], ["bank0"], ["ls01"])
     lsk = ["ls00", "ls01", "ls02", "xs"]
     l0k = ["l0", "xs"]
@@ -220,30 +266,30 @@ def rank_program(g, core, T, topo):
             vcopy(out, src, lsk, [key])
         else:
             act(out, src, lsk, [key])
-    slot0("V", 0, 0, 12, "snd0a")
-    slot0("S", 0, 12, 24, "snd0b")
-    slot0("V", 1, 0, 24, "snd0c")
-    slot0("S", 2, 0, 24, "snd0d")
+    slot0("V", 2, 24 - RW // 16, 24, "snd0a")
+    slot0("S", 2, 0, 24 - RW // 16, "snd0b")
+    slot0("V", 0, 0, 24, "snd0c")
+    slot0("S", 1, 0, 24, "snd0d")
+    at = [topo.addr(ranks[d])[:2] for d in dests]
 
-    def send(out, srcs, sem, keys, pair):
-        at = [topo.addr(ranks[d])[:2] for d in dests]
+    def fused(out, srcs, sem, keys):
+        two = [RemoteDMATransfer(dst_ids=[DstId(rid=at[j][0], pnc=at[j][1])], dma_engine_mask=_mask(share(core, ranks[dests[j]], j)),
+                                 remote_sem=T.sem[sem], srcs=[srcs[j]], dsts=[out], alu_op=0) for j in range(2)]
+        op("G", lambda: g.remote_dma_fused(two, local_sem=T.sem.sent), keys, [], signal=False)
+        nsent[0] += nout[0] + nout[1]
 
-        def mask(j, i):
-            return sum(1 << e for e in share(core, ranks[dests[j]], i))
-        alone = 3 - sum(pair)
-        two = [RemoteDMATransfer(dst_ids=[DstId(rid=at[j][0], pnc=at[j][1])], dma_engine_mask=mask(j, i), remote_sem=T.sem[sem], srcs=[srcs[j]], dsts=[out], alu_op=0) for i, j in enumerate(pair)]
+    def single(out, src, sem, keys):
+        op("G", lambda: g.remote_dma(out, src, T.sem[sem], T.sem.sent, at[2][1], at[2][0], _mask(share(core, ranks[dests[2]], 2))), keys, [], signal=False)
+        nsent[0] += nout[2]
 
-        def fused():
-            op("G", lambda: g.remote_dma_fused(two, local_sem=T.sem.sent), keys[pair[0]] + keys[pair[1]], [], signal=False)
-
-        def single():
-            op("G", lambda: g.remote_dma(out, srcs[alone], T.sem[sem], T.sem.sent, at[alone][1], at[alone][0], mask(alone, 2)), keys[alone], [], signal=False)
-        for f in ((single, fused) if alone == 0 else (fused, single)):
-            f()
+    def relay(j, src, keys):
+        rid, pid = topo.addr(helper)[:2]
+        op("G", lambda: g.remote_dma(T["hop%d" % j][:], src, T.sem["hop%d" % j], T.sem.sent, pid, rid, _mask(inner)), keys, [], signal=False)
+        nsent[0] += len(inner)
     c0 = 24 * (64 + 16 * r)
-    send(T.win0[:, c0:c0 + 384], [T.snd0[:, 384 * j:384 * j + 384] for j in range(3)], "arr0", [["snd0a", "snd0b"], ["snd0c"], ["snd0d"]], (1, 2))
-    iota(T.bcol[:], [[-16, 2]], -15, 0, "bcol")
-    iota(T.c8[:], [[0, 2], [16, 16], [4, 3]], 248, 0, "c8a")
+    relay(0, T.snd0[:, 1152 - RW:1152], ["snd0a"])
+    single(T.win0[:, c0:c0 + 384 - RW], T.snd0[:, 768:1152 - RW], "arr0", ["snd0b"])
+    fused(T.win0[:, c0:c0 + 384], [T.snd0[:, 384 * j:384 * j + 384] for j in range(2)], "arr0", ["snd0c", "snd0d"])
 
     def own(e, a, b, key):
         src, out = T.xs[:].indirect(T.l0[:, a:b]), T.win0[:, 16 * a:16 * b]
@@ -252,66 +298,63 @@ def rank_program(g, core, T, topo):
         else:
             act(out, src, l0k, [key])
     vcopy(T.l0[:], bank(1)[:, 0:96], ["bank1"], ["l0"])
-    tile(T.sgx[:, 0, :], "cqg", gc, "sgx0", ["cf"], pc)
-    tile(T.sgx[:, 1, :], "cqg", gc, "sgx1", ["cf", "c_p8"], col("p8"))
-    act(T.w3[:, 0, :], low, ["low"], ["w3l"], 3.0)
-    act(T.w3[:, 1, :], high, ["high"], ["w3h"], 3.0)
-    own("V", 0, 8, "win0a")
-    own("S", 72, 96, "win0b")
     vcopy(T.mu[:, 0:4], T.iact[:], ["iact"], ["mua"])
     ts(T.mu[:, 4:8], T.iact[:], 24.0, None, A.add, None, ["iact"], ["mub"])
     vcopy(T.cp[:, 0:24], T.ctn[:, 0, :], ["ctn0"], ["cpa"])
     ts(T.cp[:, 24:48], T.ctn[:, 1, :], col("big"), None, A.add, None, ["ctn1", "c_big"], ["cpb"])
-    muk, cpk = ["mua", "mub"], ["cpa", "cpb"]
-    tt(T.ohw[:], T.cp[:].indirect(T.mu[:]), T.a0s[:], A.is_equal, cpk + muk + ["a0s"], ["ohw"])
-    act(T.cpo[:], T.cp[:].indirect(T.pu[:]), cpk + puk, ["cpo"])
     for y in range(2):
         vcopy(T.cfb[:, y::2, :], T.ctn[:, :, 8 * y:8 * y + 16], ctk, ["cf%d" % y])
+    muk, cpk = ["mua", "mub"], ["cpa", "cpb"]
+    own("S", 80, 96, "win0b")
+    tt(T.ohw[:], T.cp[:].indirect(T.mu[:]), T.a0s[:], A.is_equal, cpk + muk + ["a0s"], ["ohw"])
     vcopy(T.nbu[:], T.inbr[:], ["inbr"], ["nbu"])
+    act(T.cpo[:], T.cp[:].indirect(T.pu[:]), cpk + puk, ["cpo"])
     for c in range(2):
         mm(2, 64 * c, 64, [(T.sgx[:, x, :], T.ohw[:, 64 * x:64 * x + 64], ["sgx%d" % x, "ohw"]) for x in range(2)])
+    act(T.ns8[:], T.cq[:].indirect(T.nbu[:]), ["cq", "nbu"], ["ns8"], 8.0)
     for j in range(8):
         out, sc = T.bd[:, :, 16 * j:16 * j + 16], T.gm[:, j:j + 1]
-        if j % 2:
+        if j < 5:
             ts(out, T.cfb[:], sc, None, A.mult, None, ["cf0", "cf1", "gm"], ["bd%d" % j])
         else:
             act(out, T.cfb[:], ["cf0", "cf1", "gm"], ["bd%d" % j], sc)
     bdk = ["bd%d" % j for j in range(8)]
     tt(T.ohz[:], T.cpo[:], bank(2)[:, 0:128], A.is_equal, ["cpo", "bank2"], ["ohz"])
-    own("V", 8, 40, "win0c")
+    own("V", 0, 40, "win0c")
 
     def rows(b, oh, key):
         for y in range(2):
             out = bank(b)[:, y, :] if b == 3 else bank(b)[:, 64 * y:64 * y + 64]
             mmo(b, out, [(T.bd[:, 2 * x + y, :], oh[:, 64 * x:64 * x + 64], bdk + [key]) for x in range(2)])
+    ev, od = T.ns8[:, 0::2], T.ns8[:, 1::2]
+
+    def base(k):
+        mm(4 + k, 0, 128, [(T.w3[:, 0, :], ev, ["w3l", "ns8"]), (T.w3[:, 1, :], od, ["w3h", "ns8"])], last=False)
+    base(0)
     rows(3, T.ohz, "ohz")
-    act(T.ns8[:], T.cq[:].indirect(T.nbu[:]), ["cq", "nbu"], ["ns8"], 8.0)
+    act(T.ms[:, 0:64], T.c48[:].indirect(T.mu[:, 0:4]), ["c48", "mua"], ["ms0"])
+    act(T.ms[:, 64:128], T.c48[:].indirect(T.mu[:, 4:8]), ["c48", "mub", "c_big"], ["ms1"], bias=col("big"))
     for n in range(2):
         act(T.rd[:, :, 64 * n:64 * n + 64], T.bank3[:, 0:2, :], ["bank3"], ["rd%d" % n])
     rdk = ["rd%d" % n for n in range(2)]
-    own("S", 60, 72, "win0d")
-    act(T.ms[:, 0:64], T.c48[:].indirect(T.mu[:, 0:4]), ["c48", "mua"], ["ms0"])
-    act(T.ms[:, 64:128], T.c48[:].indirect(T.mu[:, 4:8]), ["c48", "mub", "c_big"], ["ms1"], bias=col("big"))
-    ev, od = T.ns8[:, 0::2], T.ns8[:, 1::2]
+    own("S", 58, 80, "win0d")
     r1e, r1o, r2e, r2o = (T.rd[:, e, o::2] for e in range(2) for o in range(2))
     turn = [((low, r1e, "low"), (up, r1o, "up")), ((low, r2e, "low"), (high, r1o, "high")), ((down, r2e, "down"), (high, r2o, "high"))]
+    base(1)
+    base(2)
     for k in range(3):
-        mm(4 + k, 0, 128, [(T.w3[:, 0, :], ev, ["w3l", "ns8"])], last=False)
         for n in range(2):
-            mm(4 + k, 64 * n, 64, [(t, rh, [key] + rdk) for t, rh, key in turn[k]], first=False, last=False)
-        mm(4 + k, 0, 128, [(T.w3[:, 1, :], od, ["w3h", "ns8"])], first=False)
-    own("V", 40, 60, "win0e")
-    act(T.id124[:], same, ["same"], ["id124"], 124.0)
+            mm(4 + k, 64 * n, 64, [(t, rh, [key] + rdk) for t, rh, key in turn[k]], first=False, last=n == 1)
+    own("V", 40, 58, "win0e")
+    act(T.id60[:], same, ["same"], ["id60"], 60.0)
     act(T.c8[:, 1::3], T.c8[:, 1::3], ["c8a", "c_h8"], ["c8b"], bias=col("h8"))
-    act(T.ss8[:], T.cq[:].indirect(T.shu[:]), ["cq", "shu"], ["ss8"], 8.0)
     mm(7, 0, 128, [(low, ev, ["low", "ns8"]), (high, od, ["high", "ns8"])])
     for j, d in enumerate(dests):
         mm(7, 128 + 8 * j, 8, [(low, T.ss8[:, 16 * d:16 * d + 16:2], ["low", "ss8"]), (high, T.ss8[:, 16 * d + 1:16 * d + 16:2], ["high", "ss8"])])
+    tt(T.oha[:], T.reln[:].indirect(T.pu[:]), T.ms[:], A.is_equal, relk + puk + ["ms0", "ms1"], ["oha"])
+    rows(2, T.oha, "oha")
     for k in range(3):
         vcopy(T.lr0[:, 128 * k:128 * k + 128], bank(4 + k)[:, 0:128], ["bank%d" % (4 + k)], ["lr0%d" % k])
-        if k == 0:
-            tt(T.oha[:], T.reln[:].indirect(T.pu[:]), T.ms[:], A.is_equal, relk + puk + ["ms0", "ms1"], ["oha"])
-            rows(2, T.oha, "oha")
 
     def last1():
         act(T.ya[:], bank(2)[:, 0:128], ["bank2"], ["ya"])
@@ -324,7 +367,7 @@ def rank_program(g, core, T, topo):
         for j in range(2):
             out, b, key = T["k%d" % (j + 1)], T.bcol[:, j:j + 1], "k%d" % (j + 1)
             op("S", lambda: s.activation(out[:], bank(5)[:, 0:96], SIGN, bias=b, scale=2.0), ["bank5", "bcol"], [key])
-        mm(6, 0, 96, [(same, T.c8[:], ["same", "c8a", "c8b"]), (same, T.kb[:], ["kb"])] + [(T.id124[:], T[k][:], ["id124", k]) for k in ("k1", "k2")])
+        mm(6, 0, 96, [(same, T.c8[:], ["same", "c8a", "c8b"]), (same, T.kb[:], ["kb"])] + [(T.id60[:], T[k][:], ["id60", k]) for k in ("k1", "k2")])
 
     hs = [slice(256 * h, 256 * h + 256) for h in range(2)]
     pb = {(0, 0): 0, (0, 1): 1, (0, 2): 2, (1, 0): 4, (1, 1): 5, (1, 2): 6}
@@ -338,10 +381,11 @@ def rank_program(g, core, T, topo):
         return T.lr0[:, c + a:c + b] if t == 0 else T.lr1[:, c + a:c + b]
 
     def keys(t, k):
-        return ["win0a", "win0b", "win0c", "win0d", "win0e", "lr0%d" % k] if t == 0 else ["f1%d0" % k, "f1%d1" % k, "lr1"]
+        return ["win0b", "win0c", "win0d", "win0e", "lr0%d" % k] if t == 0 else ["f1%d0" % k, "f1%d1" % k, "lr1"]
 
     def arrived(e, t, k):
-        wait(e, "arr0" if t == 0 else "arr1k%d" % k, nin)
+        name = "arr0" if t == 0 else "arr1k%d" % k
+        wait(e, name, narr[name])
 
     def buf(n, t, k):
         return T["%s%d%d" % (n, t, k)]
@@ -360,7 +404,7 @@ def rank_program(g, core, T, topo):
     def gather(t, k, n, halves=(0, 1)):
         arrived("S", t, k)
         nm = "g" + "ab"[n]
-        whole = t == 0 and k > 0
+        whole = t == 0 and k > 0 and len(halves) == 2
         if whole:
             act(buf(nm, t, k)[:], win(t, k).indirect(lst(t, k, n)), keys(t, k), [bk(nm, t, k, 0), bk(nm, t, k, 1)])
         for h in halves:
@@ -372,91 +416,122 @@ def rank_program(g, core, T, topo):
             elif n == 1:
                 mm(pb[t, k], 256 * h, 256, [(T.idf[:], buf(nm, t, k)[:, hs[h]], ["idf", bk(nm, t, k, h)])])
 
-    def result(t, k, h):
-        if t == 0:
-            return T.win1[:, 1024 * k + 256 * h:1024 * k + 256 * h + 256], "f1%d%d" % (k, h)
-        return T["n1" + "ab"[h]][:, 256 * k:256 * k + 256], "n1%d%d" % (h, k)
+    def result(k, h):
+        return T.win1[:, 1024 * k + 256 * h:1024 * k + 256 * h + 256], "f1%d%d" % (k, h)
 
     def part(t, k, n, h):
         arrived("V", t, k)
         src, dst = {2: ("ga", "ma"), 3: ("ma", "mb"), 1: ("mb", "")}[n]
-        out, key = result(t, k, h) if n == 1 else (buf(dst, t, k)[:, hs[h]], bk(dst, t, k, h))
+        out, key = result(k, h) if n == 1 else (buf(dst, t, k)[:, hs[h]], bk(dst, t, k, h))
         tt(out, win(t, k).indirect(lst(t, k, n, 16 * h, 16 * h + 16)), buf(src, t, k)[:, hs[h]], A.max, keys(t, k) + [bk(src, t, k, h)], [key])
 
-    def join(t, k, h):
-        out, key = result(t, k, h)
-        b = pcopy.get((t, k, h), pb[t, k])
-        tt(out, bank(b)[:, hs[h]], buf("mb", t, k)[:, hs[h]], A.max, ["bank%d" % b, bk("mb", t, k, h)], [key])
+    def join(k, h):
+        out, key = result(k, h)
+        b = pb[0, k]
+        tt(out, bank(b)[:, hs[h]], buf("mb", 0, k)[:, hs[h]], A.max, ["bank%d" % b, bk("mb", 0, k, h)], [key])
 
     both, one = (0, 1), (1,)
     moved = {(0, 0): one, (0, 1): both, (0, 2): both, (1, 0): (1, 0), (1, 1): (1, 0), (1, 2): one}
 
-    def vector(t, order):
-        for k, n, h in order:
-            if n == 1 and h in moved[t, k]:
-                join(t, k, h)
-            else:
-                part(t, k, n, h)
-
-    def block(k):
-        return [(k, n, h) for n in (2, 3, 1) for h in range(2)]
+    def block0(k):
+        for n in (2, 3, 1):
+            if k == 0 and n == 1:
+                ts(T.ls1[:], bank(7)[:, 128:152], k8, None, A.add, None, ["bank7", "cf"], ["ls1"])
+            if k == 1 and n == 1:
+                ts(T.lr1[:], bank(7)[:, 0:128], k8, None, A.add, None, ["bank7", "cf"], ["lr1"])
+            for h in range(2):
+                if n == 1 and h in moved[0, k]:
+                    join(k, h)
+                else:
+                    part(0, k, n, h)
 
     def slots1(k):
         w, ky = T.win1[:, 1024 * k:1024 * k + 512], ["f1%d0" % k, "f1%d1" % k, "ls1"]
+        c1 = 1024 * k + 8 * (64 + 16 * r)
+        out, srcs = T.win1[:, c1:c1 + 128], [T.snd1[:, k, 128 * j:128 * j + 128] for j in range(3)]
         if k < 2:
-            act(T.snd1[:, k, :], w.indirect(T.ls1[:]), ky, ["snd1%d" % k])
-            kk = [["snd1%d" % k]] * 3
+            act(srcs[2], w.indirect(T.ls1[:, 16:24]), ky, ["snd1%dr" % k])
+            act(T.snd1[:, k, 0:256], w.indirect(T.ls1[:, 0:16]), ky, ["snd1%d" % k])
+            relay(1 + k, srcs[2], ["snd1%dr" % k])
+            fused(out, srcs, "arr1k%d" % k, ["snd1%d" % k])
         else:
-            act(T.snd1[:, k, 0:128], w.indirect(T.ls1[:, 0:8]), ky, ["snd12a"])
-            for j, key in ((1, "snd12b"), (2, "snd12c")):
-                vcopy(T.snd1[:, k, 128 * j:128 * j + 128], w.indirect(T.ls1[:, 8 * j:8 * j + 8]), ky, [key])
-            kk = [["snd12a"], ["snd12b"], ["snd12c"]]
-        c0 = 1024 * k + 8 * (64 + 16 * r)
-        send(T.win1[:, c0:c0 + 128], [T.snd1[:, k, 128 * j:128 * j + 128] for j in range(3)], "arr1k%d" % k, kk, (0, 1))
+            vcopy(T.lf[:], bank(6)[:, 0:96], ["bank6"], ["lf"])
+            vcopy(T.snd1[:, k, 0:256], w.indirect(T.ls1[:, 0:16]), ky, ["snd12a"])
+            vcopy(srcs[2], w.indirect(T.ls1[:, 16:24]), ky, ["snd12c"])
+            fused(out, srcs, "arr1k2", ["snd12a"])
+            single(out, srcs[2], "arr1k2", ["snd12c"])
 
     first("S", 0, 0, 0)
     first("V", 0, 0, 1)
-    ts(T.lr1[:], bank(7)[:, 0:128], k8, None, A.add, None, ["bank7", "cf"], ["lr1"])
-    ts(T.ls1[:], bank(7)[:, 128:152], k8, None, A.add, None, ["bank7", "cf"], ["ls1"])
     gather(0, 0, 1, moved[0, 0])
     gather(0, 1, 1, moved[0, 1])
     last1()
     gather(0, 1, 0)
-    gather(0, 2, 1, moved[0, 2])
-    vector(0, block(0))
+    gather(0, 2, 1, (0,))
+    block0(0)
     slots1(0)
     gather(0, 2, 0)
-    vector(0, block(1))
+    gather(0, 2, 1, (1,))
+    block0(1)
     slots1(1)
     last2()
-    vector(0, block(2))
-    slots1(2)
-    vcopy(T.lf[:], bank(6)[:, 0:96], ["bank6"], ["lf"])
-    first("V", 1, 0, 1)
+    block0(2)
     first("S", 1, 0, 0)
+    first("S", 1, 0, 1)
+    slots1(2)
     gather(1, 0, 1, moved[1, 0])
     for k in range(1, 3):
         gather(1, k, 0)
         gather(1, k, 1, moved[1, k])
-    vector(1, block(0))
-    vector(1, [(1, 2, 0), (1, 2, 1), (1, 3, 0), (1, 3, 1), (1, 1, 0), (2, 2, 0), (1, 1, 1), (2, 3, 0), (2, 1, 0), (2, 2, 1), (2, 3, 1), (2, 1, 1)])
 
-    nst = [0]
+    def quarter(k, n, u):
+        h, c = u // 2, slice(128 * u, 128 * u + 128)
+        arrived("V", 1, k)
+        out, key = T["n1q%d" % u][:, 128 * k:128 * k + 128], "n1q%d%d" % (u, k)
+
+        def mk(nm):
+            return bk(nm, 1, k, h) if k < 2 or nm[0] == "g" else "%sq%d" % (nm, u)
+        if n == 1 and h in moved[1, k]:
+            b = pcopy.get((1, k, h), pb[1, k])
+            tt(out, bank(b)[:, c], buf("mb", 1, k)[:, c], A.max, ["bank%d" % b, mk("mb")], [key])
+            return
+        src, dst = {2: ("ga", "ma"), 3: ("ma", "mb"), 1: ("mb", "")}[n]
+        if n != 1:
+            out, key = buf(dst, 1, k)[:, c], mk(dst)
+        tt(out, win(1, k).indirect(lst(1, k, n, 8 * u, 8 * u + 8)), buf(src, 1, k)[:, c], A.max, keys(1, k) + [mk(src)], [key])
 
     def final(e, a, b):
-        h = 0 if b <= 48 else 1
-        out, src = T.yo[:, 16 * a:16 * b], T["n1" + "ab"[h]][:].indirect(T.lf[:, a:b])
-        ky = ["lf"] + ["n1%d%d" % (h, k) for k in range(3)]
+        u = a // 24
+        out, src = T.yo[:, 16 * a:16 * b], T["n1q%d" % u][:].indirect(T.lf[:, a:b])
+        ky = ["lf"] + ["n1q%d%d" % (u, k) for k in range(3)]
         if e == "V":
             vcopy(out, src, ky, ["yo%d" % a])
         else:
             act(out, src, ky, ["yo%d" % a])
-        op("Y", lambda: g.sync.dma_start(T.y[:, 16 * a:16 * b], T.yo[:, 16 * a:16 * b]), ["yo%d" % a], [], "st%d" % nst[0], 16)
-        nst[0] += 1
+
+    def store(u, ks):
+        op("Y", lambda: g.sync.dma_start(T.y[:, 384 * u:384 * u + 384], T.yo[:, 384 * u:384 * u + 384]), ["yo%d" % a for a in ks], [], "st%d" % u, 16)
+    for k in range(2):
+        for n in (2, 3):
+            for h in range(2):
+                part(1, k, n, h)
+        if k == 0:
+            for u in range(4):
+                quarter(0, 1, u)
+    for k, n, u in [(1, 1, 0), (1, 1, 1), (2, 2, 0), (2, 2, 1), (2, 3, 0), (2, 3, 1), (2, 1, 0), (2, 2, 2), (2, 1, 1), (2, 3, 2),
+                    (1, 1, 2), (2, 2, 3), (2, 1, 2), (1, 1, 3), (2, 3, 3)]:
+        quarter(k, n, u)
+    final("V", 48, 56)
+    quarter(2, 1, 3)
     final("S", 0, 24)
+    store(0, [0])
     final("S", 24, 48)
-    final("V", 48, 72)
-    final("S", 72, 96)
+    store(1, [24])
+    final("S", 56, 72)
+    store(2, [48, 56])
+    final("V", 72, 84)
+    final("S", 84, 96)
+    store(3, [72, 84])
     for name in sorted(cnt):
         wait("Y", name, cnt[name])
-    wait("G", "sent", (1 + 3) * nout)
+    wait("G", "sent", nsent[0])

@@ -1,9 +1,8 @@
-import numpy as np
 from concourse.bass import DstId, RemoteDMATransfer
-from concourse.mybir import dt, AluOpType, AxisListType, ActivationFunctionType
+from concourse.mybir import AluOpType, ActivationFunctionType
 
 F, B, I, U = "float32", "bfloat16", "int32", "uint16"
-RW = 160
+RW = 192
 
 
 def _s(cols, d):
@@ -24,7 +23,7 @@ SCRATCH = {
     "ls0": _s(96, U), "l0": _s(96, U), "lr0": _s(384, U), "lr1": _s(128, U), "ls1": _s(24, U),
     "kb": _s(96, B), "k1": _s(96, B), "k2": _s(96, B), "lf": _s(96, U),
     "snd0": _s(1152, F), "snd1": _s([3, 384], F), "win0": _s(3072, F), "win1": _s(3072, F),
-    "n1q0": _s(384, F), "n1q1": _s(384, F), "n1q2": _s(384, F), "n1q3": _s(384, F), "yo": _s(1536, F),
+    "n1h0": _s(768, F), "n1h1": _s(768, F), "yo": _s(1536, F),
     "hop0": _s(RW, F), "hop1": _s(128, F), "hop2": _s(128, F),
 }
 for _t in range(2):
@@ -33,7 +32,7 @@ for _t in range(2):
             SCRATCH["%s%d%d" % (_n, _t, _k)] = _s(512, F)
 for _b in range(8):
     SCRATCH["bank%d" % _b] = ("psum", [128, 8, 64] if _b == 3 else [128, 512], F)
-SEMAPHORES = ["cv", "cs", "cte", "cg", "arr0", "arr1k0", "arr1k1", "arr1k2", "sent", "hop0", "hop1", "hop2"] + ["ld%d" % i for i in range(10)] + ["st%d" % i for i in range(8)]
+SEMAPHORES = ["cv", "cs", "cte", "cg", "arr0", "arr1k0", "arr1k1", "arr1k2", "sent", "hop0", "hop1", "hop2", "arrc"] + ["ld%d" % i for i in range(10)] + ["st%d" % i for i in range(8)]
 AF = ActivationFunctionType
 COPY, IDENT, SIGN = AF.Copy, AF.Identity, AF.Sign
 A = AluOpType
@@ -180,10 +179,10 @@ def rank_program(g, core, T, topo):
     op("S", lambda: s.dma_start(T.ipo[:], T.pose[:]), [], ["ipo"], "ld1", 16)
     op("Y", lambda: g.sync.dma_start(T.reln[:, 24:48], T.rel[:, 192:576]), [], ["relB"], "ld2", 16)
     op("S", lambda: s.dma_start(T.ish[:], T.shown[:]), [], ["ish"], "ld3", 16)
+    yc = r % 2
+    op("S", lambda: s.dma_start(T.ctn[:, yc, :], T.ct[:, 192 * yc:192 * yc + 384]), [], ["ctn%d" % yc], "ld6", 16)
     op("Y", lambda: g.sync.dma_start(T.xs[:], T.x[:]), [], ["xs"], "ld4", 16)
     op("Y", lambda: g.sync.dma_start(T.iact[:], T.act[:]), [], ["iact"], "ld5", 16)
-    for y in range(2):
-        op("Y", lambda: g.sync.dma_start(T.ctn[:, y, :], T.ct[:, 192 * y:192 * y + 384]), [], ["ctn%d" % y], "ld%d" % (6 + y), 16)
     op("Y", lambda: g.sync.dma_start(T.inbr[:], T.nbr[:]), [], ["inbr"], "ld8", 16)
     relk, ctk = ["relA", "relB"], ["ctn0", "ctn1"]
 
@@ -199,7 +198,7 @@ def rank_program(g, core, T, topo):
     iota(T.c48[:], [[0, 2], [1, 24]], 0, 0, "c48")
     iota(T.cqg[:], [[1, 8], [0, 16]], 0, 0, "cqg")
     iota(T.bcol[:], [[-16, 2]], -15, 0, "bcol")
-    iota(T.c8[:], [[0, 4], [16, 8], [4, 3]], 120, 0, "c8a")
+    iota(T.c8[:], [[0, 4], [16, 8], [4, 3]], 248, 0, "c8a")
     op("V", lambda: v.tensor_scalar(T.ci[:, 0:1], T.pi[:], 4, None, A.arith_shift_right), ["pi"], ["ci0"])
     op("V", lambda: v.tensor_scalar(T.ci[:, 1:2], T.pi[:], 15, None, A.bitwise_and), ["pi"], ["ci1"])
     op("V", lambda: v.tensor_scalar(T.ci[:, 2:3], T.pi[:], 3, 1, A.arith_shift_right, A.bitwise_and), ["pi"], ["ci2"])
@@ -255,6 +254,8 @@ def rank_program(g, core, T, topo):
     act(T.w3[:, 0, :], low, ["low"], ["w3l"], 3.0)
     act(T.w3[:, 1, :], high, ["high"], ["w3h"], 3.0)
     act(T.ss8[:], T.cq[:].indirect(T.shu[:]), ["cq", "shu"], ["ss8"], 8.0)
+    act(T.id60[:], same, ["same"], ["id60"], 124.0)
+    act(T.c8[:, 1::3], T.c8[:, 1::3], ["c8a", "c_h8"], ["c8b"], bias=col("h8"))
     vcopy(T.ls0[:, 1::3], bank(0)[:, 0:32], ["bank0"], ["ls01"])
     lsk = ["ls00", "ls01", "ls02", "xs"]
     l0k = ["l0", "xs"]
@@ -272,9 +273,12 @@ def rank_program(g, core, T, topo):
     slot0("S", 1, 0, 24, "snd0d")
     at = [topo.addr(ranks[d])[:2] for d in dests]
 
+    def transfer(to, es, sem, src, out):
+        return RemoteDMATransfer(dst_ids=[DstId(rid=to[0], pnc=to[1])], dma_engine_mask=_mask(es), remote_sem=T.sem[sem],
+                                 srcs=[src], dsts=[out], alu_op=0)
+
     def fused(out, srcs, sem, keys):
-        two = [RemoteDMATransfer(dst_ids=[DstId(rid=at[j][0], pnc=at[j][1])], dma_engine_mask=_mask(share(core, ranks[dests[j]], j)),
-                                 remote_sem=T.sem[sem], srcs=[srcs[j]], dsts=[out], alu_op=0) for j in range(2)]
+        two = [transfer(at[j], share(core, ranks[dests[j]], j), sem, srcs[j], out) for j in range(2)]
         op("G", lambda: g.remote_dma_fused(two, local_sem=T.sem.sent), keys, [], signal=False)
         nsent[0] += nout[0] + nout[1]
 
@@ -287,8 +291,11 @@ def rank_program(g, core, T, topo):
         op("G", lambda: g.remote_dma(T["hop%d" % j][:], src, T.sem["hop%d" % j], T.sem.sent, pid, rid, _mask(inner)), keys, [], signal=False)
         nsent[0] += len(inner)
     c0 = 24 * (64 + 16 * r)
-    relay(0, T.snd0[:, 1152 - RW:1152], ["snd0a"])
-    single(T.win0[:, c0:c0 + 384 - RW], T.snd0[:, 768:1152 - RW], "arr0", ["snd0b"])
+    single(T.ctn[:, yc, :], T.ctn[:, yc, :], "arrc", ["ctn%d" % yc])
+    pair = [transfer(topo.addr(helper)[:2], inner, "hop0", T.snd0[:, 1152 - RW:1152], T.hop0[:]),
+            transfer(at[2], share(core, ranks[dests[2]], 2), "arr0", T.snd0[:, 768:1152 - RW], T.win0[:, c0:c0 + 384 - RW])]
+    op("G", lambda: g.remote_dma_fused(pair, local_sem=T.sem.sent), ["snd0a", "snd0b"], [], signal=False)
+    nsent[0] += len(inner) + nout[2]
     fused(T.win0[:, c0:c0 + 384], [T.snd0[:, 384 * j:384 * j + 384] for j in range(2)], "arr0", ["snd0c", "snd0d"])
 
     def own(e, a, b, key):
@@ -297,21 +304,23 @@ def rank_program(g, core, T, topo):
             vcopy(out, src, l0k, [key])
         else:
             act(out, src, l0k, [key])
+    for j, d in enumerate(dests):
+        mm(7, 128 + 8 * j, 8, [(low, T.ss8[:, 16 * d:16 * d + 16:2], ["low", "ss8"]), (high, T.ss8[:, 16 * d + 1:16 * d + 16:2], ["high", "ss8"])])
     vcopy(T.l0[:], bank(1)[:, 0:96], ["bank1"], ["l0"])
+    vcopy(T.nbu[:], T.inbr[:], ["inbr"], ["nbu"])
     vcopy(T.mu[:, 0:4], T.iact[:], ["iact"], ["mua"])
     ts(T.mu[:, 4:8], T.iact[:], 24.0, None, A.add, None, ["iact"], ["mub"])
+    wait("V", "arrc", nin[2])
     vcopy(T.cp[:, 0:24], T.ctn[:, 0, :], ["ctn0"], ["cpa"])
     ts(T.cp[:, 24:48], T.ctn[:, 1, :], col("big"), None, A.add, None, ["ctn1", "c_big"], ["cpb"])
     for y in range(2):
         vcopy(T.cfb[:, y::2, :], T.ctn[:, :, 8 * y:8 * y + 16], ctk, ["cf%d" % y])
     muk, cpk = ["mua", "mub"], ["cpa", "cpb"]
-    own("S", 80, 96, "win0b")
+    act(T.ns8[:], T.cq[:].indirect(T.nbu[:]), ["cq", "nbu"], ["ns8"], 8.0)
     tt(T.ohw[:], T.cp[:].indirect(T.mu[:]), T.a0s[:], A.is_equal, cpk + muk + ["a0s"], ["ohw"])
-    vcopy(T.nbu[:], T.inbr[:], ["inbr"], ["nbu"])
     act(T.cpo[:], T.cp[:].indirect(T.pu[:]), cpk + puk, ["cpo"])
     for c in range(2):
         mm(2, 64 * c, 64, [(T.sgx[:, x, :], T.ohw[:, 64 * x:64 * x + 64], ["sgx%d" % x, "ohw"]) for x in range(2)])
-    act(T.ns8[:], T.cq[:].indirect(T.nbu[:]), ["cq", "nbu"], ["ns8"], 8.0)
     for j in range(8):
         out, sc = T.bd[:, :, 16 * j:16 * j + 16], T.gm[:, j:j + 1]
         if j < 5:
@@ -320,7 +329,7 @@ def rank_program(g, core, T, topo):
             act(out, T.cfb[:], ["cf0", "cf1", "gm"], ["bd%d" % j], sc)
     bdk = ["bd%d" % j for j in range(8)]
     tt(T.ohz[:], T.cpo[:], bank(2)[:, 0:128], A.is_equal, ["cpo", "bank2"], ["ohz"])
-    own("V", 0, 40, "win0c")
+    own("V", 0, 36, "win0c")
 
     def rows(b, oh, key):
         for y in range(2):
@@ -334,10 +343,11 @@ def rank_program(g, core, T, topo):
     rows(3, T.ohz, "ohz")
     act(T.ms[:, 0:64], T.c48[:].indirect(T.mu[:, 0:4]), ["c48", "mua"], ["ms0"])
     act(T.ms[:, 64:128], T.c48[:].indirect(T.mu[:, 4:8]), ["c48", "mub", "c_big"], ["ms1"], bias=col("big"))
+    own("S", 80, 96, "win0b")
     for n in range(2):
         act(T.rd[:, :, 64 * n:64 * n + 64], T.bank3[:, 0:2, :], ["bank3"], ["rd%d" % n])
     rdk = ["rd%d" % n for n in range(2)]
-    own("S", 58, 80, "win0d")
+    own("S", 54, 80, "win0d")
     r1e, r1o, r2e, r2o = (T.rd[:, e, o::2] for e in range(2) for o in range(2))
     turn = [((low, r1e, "low"), (up, r1o, "up")), ((low, r2e, "low"), (high, r1o, "high")), ((down, r2e, "down"), (high, r2o, "high"))]
     base(1)
@@ -345,12 +355,8 @@ def rank_program(g, core, T, topo):
     for k in range(3):
         for n in range(2):
             mm(4 + k, 64 * n, 64, [(t, rh, [key] + rdk) for t, rh, key in turn[k]], first=False, last=n == 1)
-    own("V", 40, 58, "win0e")
-    act(T.id60[:], same, ["same"], ["id60"], 60.0)
-    act(T.c8[:, 1::3], T.c8[:, 1::3], ["c8a", "c_h8"], ["c8b"], bias=col("h8"))
+    own("V", 36, 54, "win0e")
     mm(7, 0, 128, [(low, ev, ["low", "ns8"]), (high, od, ["high", "ns8"])])
-    for j, d in enumerate(dests):
-        mm(7, 128 + 8 * j, 8, [(low, T.ss8[:, 16 * d:16 * d + 16:2], ["low", "ss8"]), (high, T.ss8[:, 16 * d + 1:16 * d + 16:2], ["high", "ss8"])])
     tt(T.oha[:], T.reln[:].indirect(T.pu[:]), T.ms[:], A.is_equal, relk + puk + ["ms0", "ms1"], ["oha"])
     rows(2, T.oha, "oha")
     for k in range(3):
@@ -370,8 +376,8 @@ def rank_program(g, core, T, topo):
         mm(6, 0, 96, [(same, T.c8[:], ["same", "c8a", "c8b"]), (same, T.kb[:], ["kb"])] + [(T.id60[:], T[k][:], ["id60", k]) for k in ("k1", "k2")])
 
     hs = [slice(256 * h, 256 * h + 256) for h in range(2)]
-    pb = {(0, 0): 0, (0, 1): 1, (0, 2): 2, (1, 0): 4, (1, 1): 5, (1, 2): 6}
-    pcopy = {(1, 0, 0): 7, (1, 1, 0): 0}
+    pb = {(0, 0): 0, (0, 1): 1, (0, 2): 2, (1, 0): 4, (1, 1): 5, (1, 2): 7}
+    pcopy = {(1, 1, 0): 0, (1, 0, 0): 1}
 
     def win(t, k):
         return T.win0[:] if t == 0 else T.win1[:, 1024 * k:1024 * k + 1024]
@@ -393,13 +399,18 @@ def rank_program(g, core, T, topo):
     def bk(n, t, k, h):
         return "%s%d%dh%d" % (n, t, k, h)
 
-    def first(e, t, k, h):
+    def first(e, t, k, h, n=0):
         arrived(e, t, k)
-        out, src, ky = buf("ga", t, k)[:, hs[h]], win(t, k).indirect(lst(t, k, 0, 16 * h, 16 * h + 16)), keys(t, k)
+        nm = "g" + "ab"[n]
+        out, src, ky = buf(nm, t, k)[:, hs[h]], win(t, k).indirect(lst(t, k, n, 16 * h, 16 * h + 16)), keys(t, k)
         if e == "V":
-            vcopy(out, src, ky, [bk("ga", t, k, h)])
+            vcopy(out, src, ky, [bk(nm, t, k, h)])
         else:
-            act(out, src, ky, [bk("ga", t, k, h)])
+            act(out, src, ky, [bk(nm, t, k, h)])
+
+    def move(t, k, h):
+        b = pcopy[t, k, h]
+        act(bank(b)[:, hs[h]], buf("gb", t, k)[:, hs[h]], [bk("gb", t, k, h)], ["bank%d" % b])
 
     def gather(t, k, n, halves=(0, 1)):
         arrived("S", t, k)
@@ -411,8 +422,7 @@ def rank_program(g, core, T, topo):
             if not whole:
                 act(buf(nm, t, k)[:, hs[h]], win(t, k).indirect(lst(t, k, n, 16 * h, 16 * h + 16)), keys(t, k), [bk(nm, t, k, h)])
             if n == 1 and (t, k, h) in pcopy:
-                b = pcopy[t, k, h]
-                act(bank(b)[:, hs[h]], buf(nm, t, k)[:, hs[h]], [bk(nm, t, k, h)], ["bank%d" % b])
+                move(t, k, h)
             elif n == 1:
                 mm(pb[t, k], 256 * h, 256, [(T.idf[:], buf(nm, t, k)[:, hs[h]], ["idf", bk(nm, t, k, h)])])
 
@@ -431,14 +441,10 @@ def rank_program(g, core, T, topo):
         tt(out, bank(b)[:, hs[h]], buf("mb", 0, k)[:, hs[h]], A.max, ["bank%d" % b, bk("mb", 0, k, h)], [key])
 
     both, one = (0, 1), (1,)
-    moved = {(0, 0): one, (0, 1): both, (0, 2): both, (1, 0): (1, 0), (1, 1): (1, 0), (1, 2): one}
+    moved = {(0, 0): one, (0, 1): both, (0, 2): both, (1, 0): (1, 0), (1, 2): one}
 
     def block0(k):
         for n in (2, 3, 1):
-            if k == 0 and n == 1:
-                ts(T.ls1[:], bank(7)[:, 128:152], k8, None, A.add, None, ["bank7", "cf"], ["ls1"])
-            if k == 1 and n == 1:
-                ts(T.lr1[:], bank(7)[:, 0:128], k8, None, A.add, None, ["bank7", "cf"], ["lr1"])
             for h in range(2):
                 if n == 1 and h in moved[0, k]:
                     join(k, h)
@@ -456,13 +462,15 @@ def rank_program(g, core, T, topo):
             fused(out, srcs, "arr1k%d" % k, ["snd1%d" % k])
         else:
             vcopy(T.lf[:], bank(6)[:, 0:96], ["bank6"], ["lf"])
-            vcopy(T.snd1[:, k, 0:256], w.indirect(T.ls1[:, 0:16]), ky, ["snd12a"])
             vcopy(srcs[2], w.indirect(T.ls1[:, 16:24]), ky, ["snd12c"])
-            fused(out, srcs, "arr1k2", ["snd12a"])
+            vcopy(T.snd1[:, k, 0:256], w.indirect(T.ls1[:, 0:16]), ky, ["snd12a"])
             single(out, srcs[2], "arr1k2", ["snd12c"])
+            fused(out, srcs, "arr1k2", ["snd12a"])
 
     first("S", 0, 0, 0)
     first("V", 0, 0, 1)
+    ts(T.ls1[:], bank(7)[:, 128:152], k8, None, A.add, None, ["bank7", "cf"], ["ls1"])
+    ts(T.lr1[:], bank(7)[:, 0:128], k8, None, A.add, None, ["bank7", "cf"], ["lr1"])
     gather(0, 0, 1, moved[0, 0])
     gather(0, 1, 1, moved[0, 1])
     last1()
@@ -480,30 +488,40 @@ def rank_program(g, core, T, topo):
     first("S", 1, 0, 1)
     slots1(2)
     gather(1, 0, 1, moved[1, 0])
-    for k in range(1, 3):
-        gather(1, k, 0)
-        gather(1, k, 1, moved[1, k])
+    gather(1, 1, 0)
+    first("S", 1, 1, 0, 1)
+    gather(1, 1, 1, one)
+    move(1, 1, 0)
+    gather(1, 2, 0)
+    gather(1, 2, 1, one)
 
-    def quarter(k, n, u):
+    def join1(k, h):
+        b = pcopy.get((1, k, h), pb[1, k])
+        tt(T["n1h%d" % h][:, 256 * k:256 * k + 256], bank(b)[:, hs[h]], buf("mb", 1, k)[:, hs[h]], A.max,
+           ["bank%d" % b, bk("mb", 1, k, h)], ["n1h%d%d" % (h, k)])
+
+    def quarter(n, u):
         h, c = u // 2, slice(128 * u, 128 * u + 128)
-        arrived("V", 1, k)
-        out, key = T["n1q%d" % u][:, 128 * k:128 * k + 128], "n1q%d%d" % (u, k)
+        arrived("V", 1, 2)
+        c2 = 512 + 128 * (u % 2)
+        out, key = T["n1h%d" % h][:, c2:c2 + 128], "n1q%d" % u
 
         def mk(nm):
-            return bk(nm, 1, k, h) if k < 2 or nm[0] == "g" else "%sq%d" % (nm, u)
-        if n == 1 and h in moved[1, k]:
-            b = pcopy.get((1, k, h), pb[1, k])
-            tt(out, bank(b)[:, c], buf("mb", 1, k)[:, c], A.max, ["bank%d" % b, mk("mb")], [key])
+            return bk(nm, 1, 2, h) if nm[0] == "g" else "%sq%d" % (nm, u)
+        if n == 1 and h in moved[1, 2]:
+            b = pb[1, 2]
+            tt(out, bank(b)[:, c], buf("mb", 1, 2)[:, c], A.max, ["bank%d" % b, mk("mb")], [key])
             return
         src, dst = {2: ("ga", "ma"), 3: ("ma", "mb"), 1: ("mb", "")}[n]
         if n != 1:
-            out, key = buf(dst, 1, k)[:, c], mk(dst)
-        tt(out, win(1, k).indirect(lst(1, k, n, 8 * u, 8 * u + 8)), buf(src, 1, k)[:, c], A.max, keys(1, k) + [mk(src)], [key])
+            out, key = buf(dst, 1, 2)[:, c], mk(dst)
+        tt(out, win(1, 2).indirect(lst(1, 2, n, 8 * u, 8 * u + 8)), buf(src, 1, 2)[:, c], A.max, keys(1, 2) + [mk(src)], [key])
 
     def final(e, a, b):
         u = a // 24
-        out, src = T.yo[:, 16 * a:16 * b], T["n1q%d" % u][:].indirect(T.lf[:, a:b])
-        ky = ["lf"] + ["n1q%d%d" % (u, k) for k in range(3)]
+        h, j = u // 2, u % 2
+        out, src = T.yo[:, 16 * a:16 * b], T["n1h%d" % h][:, 128 * j:128 * j + 640].indirect(T.lf[:, a:b])
+        ky = ["lf", "n1h%d0" % h, "n1h%d1" % h] + ["n1q%d" % w for w in range(2 * h, u + 1)]
         if e == "V":
             vcopy(out, src, ky, ["yo%d" % a])
         else:
@@ -515,14 +533,16 @@ def rank_program(g, core, T, topo):
         for n in (2, 3):
             for h in range(2):
                 part(1, k, n, h)
+        join1(k, 0)
         if k == 0:
-            for u in range(4):
-                quarter(0, 1, u)
-    for k, n, u in [(1, 1, 0), (1, 1, 1), (2, 2, 0), (2, 2, 1), (2, 3, 0), (2, 3, 1), (2, 1, 0), (2, 2, 2), (2, 1, 1), (2, 3, 2),
-                    (1, 1, 2), (2, 2, 3), (2, 1, 2), (1, 1, 3), (2, 3, 3)]:
-        quarter(k, n, u)
+            join1(0, 1)
+    for n, u in [(2, 0), (2, 1), (3, 0), (3, 1), (1, 0), (2, 2), (1, 1), (3, 2), (2, 3), (0, 1), (1, 2), (3, 3)]:
+        if n == 0:
+            join1(1, u)
+        else:
+            quarter(n, u)
     final("V", 48, 56)
-    quarter(2, 1, 3)
+    quarter(1, 3)
     final("S", 0, 24)
     store(0, [0])
     final("S", 24, 48)

from concourse.bass import DstId, RemoteDMATransfer
from concourse.mybir import AluOpType, ActivationFunctionType

F, B, I, U = "float32", "bfloat16", "int32", "uint16"
RW = 192


def _s(cols, d):
    return ("sbuf", [128] + (cols if isinstance(cols, list) else [cols]), d)


SCRATCH = {
    "xs": _s(1536, F), "ipo": _s(4, I), "ish": _s(4, I), "iact": _s(4, I), "inbr": _s(16, I), "reln": _s(48, I),
    "ctn": _s([2, 24], I),
    "pi": _s(1, I), "ci": _s(4, I), "cf": _s(4, F), "cc": _s(16, F), "pcols": _s(3, F), "bcol": _s(2, F),
    "cq": _s(128, B), "cqg": _s(128, B), "c48": _s(48, B), "i24": _s(128, F), "c8": _s(96, B), "id60": _s(128, B),
    "c5": _s(640, B), "sgx": _s([2, 128], B), "w3": _s([2, 128], B), "gm": _s(8, F),
    "idf": _s(128, F), "sd32": _s(128, F), "su32": _s(128, F),
    "pu": _s(8, U), "mu": _s(8, U), "shu": _s(4, U), "nbu": _s(16, U),
    "X": _s(128, F), "xs0": _s(64, F), "xs1": _s(64, F), "cp": _s(48, F), "cfb": _s([4, 16], B), "bd": _s([4, 128], B),
    "a0s": _s(128, F), "ms": _s(128, F), "cpo": _s(128, F), "ohw": _s(128, B), "ohz": _s(128, B), "oha": _s(128, B),
    "rd": _s([2, 128], B), "ya": _s(128, B), "ns8": _s(256, B), "ss8": _s(64, B),
    "ls0": _s(96, U), "l0": _s(96, U), "lr0": _s(384, U), "lr1": _s(128, U), "ls1": _s(24, U),
    "kb": _s(96, B), "k1": _s(96, B), "k2": _s(96, B), "lf": _s(96, U),
    "snd0": _s(1152, F), "snd1": _s([3, 384], F), "win0": _s(3072, F), "win1": _s(3072, F),
    "n1h0": _s(768, F), "n1h1": _s(768, F), "yo": _s(1536, F),
    "hop0": _s(RW, F), "hop1": _s(128, F), "hop2": _s(128, F),
}
for _t in range(2):
    for _k in range(3):
        for _n in ("ga", "gb", "ma", "mb"):
            SCRATCH["%s%d%d" % (_n, _t, _k)] = _s(512, F)
for _b in range(8):
    SCRATCH["bank%d" % _b] = ("psum", [128, 8, 64] if _b == 3 else [128, 512], F)
SEMAPHORES = ["cv", "cs", "cte", "cg", "arr0", "arr1k0", "arr1k1", "arr1k2", "sent", "hop0", "hop1", "hop2", "arrc"] + ["ld%d" % i for i in range(10)] + ["st%d" % i for i in range(8)]
AF = ActivationFunctionType
COPY, IDENT, SIGN = AF.Copy, AF.Identity, AF.Sign
A = AluOpType


def _queues(g, T):
    q = {"V": g.vector, "S": g.scalar, "T": g.tensor, "G": g, "Y": g.sync}
    csem = {"V": "cv", "S": "cs", "T": "cte", "G": "cg"}
    cnt = {}
    known = {e: {} for e in q}
    wrote, read = {}, {}

    def after(e, tok):
        sem, val, snap = tok[1], tok[2], tok[3]
        if known[e].get(sem, 0) < val:
            q[e].wait_ge(T.sem[sem], val)
            known[e][sem] = val
            for s, v in snap.items():
                if known[e].get(s, 0) < v:
                    known[e][s] = v

    def op(e, fn, reads=(), writes=(), sem=None, inc=1, signal=True):
        toks = []
        for k in reads:
            if k in wrote:
                toks.append(wrote[k])
            if k.startswith("bank"):
                toks += [t for t in read.get(k, []) if t[0] != e]
        for k in writes:
            if k in wrote and not (e == "T" and wrote[k][0] == "T"):
                toks.append(wrote[k])
            toks += [t for t in read.get(k, []) if t[0] != e]
        best = {}
        for t in toks:
            if t[1] not in best or best[t[1]][2] < t[2]:
                best[t[1]] = t
        for t in best.values():
            after(e, t)
        ins = fn()
        if not signal:
            return
        name = sem or csem[e]
        cnt[name] = cnt.get(name, 0) + inc
        ins.then_inc(T.sem[name], inc)
        tok = (e, name, cnt[name], dict(known[e]))
        for k in reads:
            read.setdefault(k, []).append(tok)
        for k in writes:
            wrote[k] = tok
            read[k] = []

    def wait(e, sem, val):
        if known[e].get(sem, 0) < val:
            q[e].wait_ge(T.sem[sem], val)
            known[e][sem] = val
    return q, op, wait, cnt


def _mask(es):
    return sum(1 << e for e in es)


def _helper(topo, ranks, r):
    c = ranks[r]
    return [h for h in topo.cores_of(c) if topo.die(h) != topo.die(c) and h not in ranks
            and all(topo.may_write(h, d) for d in ranks if d != c)][0]


def _inner(topo, ranks, r):
    out = topo.engines(ranks[r], ranks[(r - 1) % len(ranks)])
    return [e for e in topo.engines(ranks[r], _helper(topo, ranks, r)) if e not in out]


def _hand_on(g, core, T, topo, ranks, r):
    d = ranks[(r - 1) % len(ranks)]
    rid, pid = topo.addr(d)[:2]
    n = len(_inner(topo, ranks, r))
    c0 = 24 * (64 + 16 * r) + 384 - RW
    outs = [(T.win0[:, c0:c0 + RW], "arr0")]
    for k in range(2):
        c1 = 1024 * k + 8 * (64 + 16 * r)
        outs.append((T.win1[:, c1:c1 + 128], "arr1k%d" % k))
    for j, (out, sem) in enumerate(outs):
        g.wait_ge(T.sem["hop%d" % j], n)
        g.remote_dma(out, T["hop%d" % j][:], T.sem[sem], T.sem.sent, pid, rid, topo.mask(core, d))
    g.wait_ge(T.sem.sent, len(outs) * len(topo.engines(core, d)))


def rank_program(g, core, T, topo):
    r = T.rank_of(core)
    ranks = list(T.cores)
    n_ranks = len(ranks)
    if r is None:
        for rr in range(n_ranks):
            if _helper(topo, ranks, rr) == core:
                _hand_on(g, core, T, topo, ranks, rr)
        return
    dests = [(r + 1 + j) % n_ranks for j in range(n_ranks - 1)]
    q, op, wait, cnt = _queues(g, T)
    v, s, te = g.vector, g.scalar, g.tensor
    helper, inner = _helper(topo, ranks, r), _inner(topo, ranks, r)

    def share(a, b, i):
        es = topo.engines(a, b)
        h = len(es) // 2
        return (es[:h], es[h:], es)[i]
    nout = [len(share(core, ranks[d], j)) for j, d in enumerate(dests)]
    nin = [len(share(ranks[(r - 1 - j) % n_ranks], core, j)) for j in range(n_ranks - 1)]
    nrel = len(topo.engines(_helper(topo, ranks, (r + 1) % n_ranks), core))
    narr = {"arr0": sum(nin) + nrel, "arr1k0": nin[0] + nin[1] + nrel, "arr1k1": nin[0] + nin[1] + nrel, "arr1k2": sum(nin)}
    nsent = [0]

    def bank(b):
        return T["bank%d" % b]

    def ts(out, in0, s1, s2, o0, o1, reads, writes):
        if o1 is None:
            op("V", lambda: v.tensor_scalar(out, in0, s1, None, o0), reads, writes)
        else:
            op("V", lambda: v.tensor_scalar(out, in0, s1, s2, o0, o1), reads, writes)

    def tt(out, a, b, o, reads, writes):
        op("V", lambda: v.tensor_tensor(out, a, b, o), reads, writes)

    def vcopy(out, a, reads, writes):
        op("V", lambda: v.tensor_copy(out, a), reads, writes)

    def act(out, a, reads, writes, scale=None, bias=None):
        if bias is not None:
            op("S", lambda: s.activation(out, a, IDENT, bias=bias), reads, writes)
        elif scale is None:
            op("S", lambda: s.activation(out, a, COPY), reads, writes)
        else:
            op("S", lambda: s.activation(out, a, COPY, scale=scale), reads, writes)

    def mmo(b, out, parts, first=True, last=True):
        for i, (l, rh, keys) in enumerate(parts):
            op("T", lambda: te.matmul(out, l, rh, first and i == 0, last and i == len(parts) - 1), keys, ["bank%d" % b])

    def mm(b, c0, n, parts, first=True, last=True):
        mmo(b, bank(b)[:, c0:c0 + n], parts, first, last)

    op("Y", lambda: g.sync.dma_start(T.reln[:, 0:24], T.rel[:, 0:384]), [], ["relA"], "ld0", 16)
    op("S", lambda: s.dma_start(T.ipo[:], T.pose[:]), [], ["ipo"], "ld1", 16)
    op("Y", lambda: g.sync.dma_start(T.reln[:, 24:48], T.rel[:, 192:576]), [], ["relB"], "ld2", 16)
    op("S", lambda: s.dma_start(T.ish[:], T.shown[:]), [], ["ish"], "ld3", 16)
    yc = r % 2
    op("S", lambda: s.dma_start(T.ctn[:, yc, :], T.ct[:, 192 * yc:192 * yc + 384]), [], ["ctn%d" % yc], "ld6", 16)
    op("Y", lambda: g.sync.dma_start(T.xs[:], T.x[:]), [], ["xs"], "ld4", 16)
    op("Y", lambda: g.sync.dma_start(T.iact[:], T.act[:]), [], ["iact"], "ld5", 16)
    op("Y", lambda: g.sync.dma_start(T.inbr[:], T.nbr[:]), [], ["inbr"], "ld8", 16)
    relk, ctk = ["relA", "relB"], ["ctn0", "ctn1"]

    def iota(out, pat, base, cm, key, flag=True):
        if flag:
            op("G", lambda: g.iota(out, pat, base, cm, allow_small_or_imprecise_dtypes=True), [], [key])
        else:
            op("G", lambda: g.iota(out, pat, base, cm), [], [key])
    iota(T.pi[:], [[1, 1]], 0, 1, "pi", False)
    iota(T.pcols[:], [[8, 3]], -8, 1, "pcols")
    iota(T.cq[:], [[1, 128]], 0, 0, "cq")
    iota(T.i24[:], [[0, 2], [24, 64]], 0, 0, "i24")
    iota(T.c48[:], [[0, 2], [1, 24]], 0, 0, "c48")
    iota(T.cqg[:], [[1, 8], [0, 16]], 0, 0, "cqg")
    iota(T.bcol[:], [[-16, 2]], -15, 0, "bcol")
    iota(T.c8[:], [[0, 4], [16, 8], [4, 3]], 248, 0, "c8a")
    op("V", lambda: v.tensor_scalar(T.ci[:, 0:1], T.pi[:], 4, None, A.arith_shift_right), ["pi"], ["ci0"])
    op("V", lambda: v.tensor_scalar(T.ci[:, 1:2], T.pi[:], 15, None, A.bitwise_and), ["pi"], ["ci1"])
    op("V", lambda: v.tensor_scalar(T.ci[:, 2:3], T.pi[:], 3, 1, A.arith_shift_right, A.bitwise_and), ["pi"], ["ci2"])
    op("V", lambda: v.tensor_scalar(T.ci[:, 3:4], T.pi[:], 7, None, A.bitwise_and), ["pi"], ["ci3"])
    vcopy(T.cf[:], T.ci[:], ["ci0", "ci1", "ci2", "ci3"], ["cf"])
    gc, pc, hc, k8 = (T.cf[:, j:j + 1] for j in range(4))
    ccn = {}

    def col(name):
        return T.cc[:, ccn[name]:ccn[name] + 1]

    def mkcol(name, src, m, a):
        ccn[name] = len(ccn)
        op("S", lambda: s.activation(col(name), src, COPY, bias=float(a), scale=float(m)), ["cf"], ["c_" + name])
    mkcol("nh", hc, -1, 1)
    mkcol("p8", pc, 1, 8)
    mkcol("big", hc, -100, 100)
    mkcol("h8", hc, 8, -4)
    colPm8, colP, colPp8 = (T.pcols[:, j:j + 1] for j in range(3))

    def tile(o1, src, s1, key, reads, s2=None):
        ts(o1, T[src][:], s1, s2, A.is_equal, A.mult if s2 is not None else None, [src] + reads, [key])
    down, same, up, low, high = (T.c5[:, 128 * j:128 * j + 128] for j in range(5))
    tile(down, "cq", colPm8, "down", ["pcols", "cf"], hc)
    tile(same, "cq", colP, "same", ["pcols"])
    tile(up, "cq", colPp8, "up", ["pcols", "c_nh"], col("nh"))
    act(T.sd32[:], down, ["down"], ["sd32"])
    act(T.idf[:], same, ["same"], ["idf"])
    act(T.su32[:], up, ["up"], ["su32"])

    vcopy(T.pu[:, 0:4], T.ipo[:], ["ipo"], ["pua"])
    ts(T.pu[:, 4:8], T.ipo[:], 24.0, None, A.add, None, ["ipo"], ["pub"])
    vcopy(T.shu[:], T.ish[:], ["ish"], ["shu"])
    puk = ["pua", "pub"]
    tt(T.X[:], T.reln[:].indirect(T.pu[:]), T.i24[:], A.add, relk + puk + ["i24"], ["X"])
    tile(low, "cq", colP, "low", ["pcols", "c_nh"], col("nh"))
    tile(high, "cq", colP, "high", ["pcols", "cf"], hc)
    vcopy(T.xs0[:], T.X[:, 0:64].indirect(T.shu[:]), ["X", "shu"], ["xs0"])
    act(T.xs1[:], T.X[:, 64:128].indirect(T.shu[:]), ["X", "shu"], ["xs1"])
    act(T.a0s[:], T.c48[:].indirect(T.pu[:]), puk + ["c48"], ["a0s"])

    def middle(b, out, d, u):
        mmo(b, out, [d, u])
    middle(0, bank(0)[:, 0:32], (T.sd32[:], T.xs1[:, 0::2], ["sd32", "xs1"]), (T.su32[:], T.xs0[:, 1::2], ["su32", "xs0"]))
    mmo(1, bank(1)[:, 0:96:3], [(T.idf[:], T.X[:, 0:64:2], ["idf", "X"])])
    middle(1, bank(1)[:, 1:96:3], (T.sd32[:], T.X[:, 64:128:2], ["sd32", "X"]), (T.su32[:], T.X[:, 1:64:2], ["su32", "X"]))
    mmo(1, bank(1)[:, 2:96:3], [(T.idf[:], T.X[:, 65:128:2], ["idf", "X"])])
    ts(T.gm[:], T.cq[:, 0:8], gc, None, A.is_equal, None, ["cq", "cf"], ["gm"])
    vcopy(T.ls0[:, 0::3], T.xs0[:, 0::2], ["xs0"], ["ls00"])
    vcopy(T.ls0[:, 2::3], T.xs1[:, 1::2], ["xs1"], ["ls02"])
    tile(T.sgx[:, 0, :], "cqg", gc, "sgx0", ["cf"], pc)
    tile(T.sgx[:, 1, :], "cqg", gc, "sgx1", ["cf", "c_p8"], col("p8"))
    act(T.w3[:, 0, :], low, ["low"], ["w3l"], 3.0)
    act(T.w3[:, 1, :], high, ["high"], ["w3h"], 3.0)
    act(T.ss8[:], T.cq[:].indirect(T.shu[:]), ["cq", "shu"], ["ss8"], 8.0)
    act(T.id60[:], same, ["same"], ["id60"], 124.0)
    act(T.c8[:, 1::3], T.c8[:, 1::3], ["c8a", "c_h8"], ["c8b"], bias=col("h8"))
    vcopy(T.ls0[:, 1::3], bank(0)[:, 0:32], ["bank0"], ["ls01"])
    lsk = ["ls00", "ls01", "ls02", "xs"]
    l0k = ["l0", "xs"]

    def slot0(e, j, a, b, key):
        c = 24 * dests[j]
        src, out = T.xs[:].indirect(T.ls0[:, c + a:c + b]), T.snd0[:, 384 * j + 16 * a:384 * j + 16 * b]
        if e == "V":
            vcopy(out, src, lsk, [key])
        else:
            act(out, src, lsk, [key])
    slot0("V", 2, 24 - RW // 16, 24, "snd0a")
    slot0("S", 2, 0, 24 - RW // 16, "snd0b")
    slot0("V", 0, 0, 24, "snd0c")
    slot0("S", 1, 0, 24, "snd0d")
    at = [topo.addr(ranks[d])[:2] for d in dests]

    def transfer(to, es, sem, src, out):
        return RemoteDMATransfer(dst_ids=[DstId(rid=to[0], pnc=to[1])], dma_engine_mask=_mask(es), remote_sem=T.sem[sem],
                                 srcs=[src], dsts=[out], alu_op=0)

    def fused(out, srcs, sem, keys):
        two = [transfer(at[j], share(core, ranks[dests[j]], j), sem, srcs[j], out) for j in range(2)]
        op("G", lambda: g.remote_dma_fused(two, local_sem=T.sem.sent), keys, [], signal=False)
        nsent[0] += nout[0] + nout[1]

    def single(out, src, sem, keys):
        op("G", lambda: g.remote_dma(out, src, T.sem[sem], T.sem.sent, at[2][1], at[2][0], _mask(share(core, ranks[dests[2]], 2))), keys, [], signal=False)
        nsent[0] += nout[2]

    def relay(j, src, keys):
        rid, pid = topo.addr(helper)[:2]
        op("G", lambda: g.remote_dma(T["hop%d" % j][:], src, T.sem["hop%d" % j], T.sem.sent, pid, rid, _mask(inner)), keys, [], signal=False)
        nsent[0] += len(inner)
    c0 = 24 * (64 + 16 * r)
    single(T.ctn[:, yc, :], T.ctn[:, yc, :], "arrc", ["ctn%d" % yc])
    pair = [transfer(topo.addr(helper)[:2], inner, "hop0", T.snd0[:, 1152 - RW:1152], T.hop0[:]),
            transfer(at[2], share(core, ranks[dests[2]], 2), "arr0", T.snd0[:, 768:1152 - RW], T.win0[:, c0:c0 + 384 - RW])]
    op("G", lambda: g.remote_dma_fused(pair, local_sem=T.sem.sent), ["snd0a", "snd0b"], [], signal=False)
    nsent[0] += len(inner) + nout[2]
    fused(T.win0[:, c0:c0 + 384], [T.snd0[:, 384 * j:384 * j + 384] for j in range(2)], "arr0", ["snd0c", "snd0d"])

    def own(e, a, b, key):
        src, out = T.xs[:].indirect(T.l0[:, a:b]), T.win0[:, 16 * a:16 * b]
        if e == "V":
            vcopy(out, src, l0k, [key])
        else:
            act(out, src, l0k, [key])
    for j, d in enumerate(dests):
        mm(7, 128 + 8 * j, 8, [(low, T.ss8[:, 16 * d:16 * d + 16:2], ["low", "ss8"]), (high, T.ss8[:, 16 * d + 1:16 * d + 16:2], ["high", "ss8"])])
    vcopy(T.l0[:], bank(1)[:, 0:96], ["bank1"], ["l0"])
    vcopy(T.nbu[:], T.inbr[:], ["inbr"], ["nbu"])
    vcopy(T.mu[:, 0:4], T.iact[:], ["iact"], ["mua"])
    ts(T.mu[:, 4:8], T.iact[:], 24.0, None, A.add, None, ["iact"], ["mub"])
    wait("V", "arrc", nin[2])
    vcopy(T.cp[:, 0:24], T.ctn[:, 0, :], ["ctn0"], ["cpa"])
    ts(T.cp[:, 24:48], T.ctn[:, 1, :], col("big"), None, A.add, None, ["ctn1", "c_big"], ["cpb"])
    for y in range(2):
        vcopy(T.cfb[:, y::2, :], T.ctn[:, :, 8 * y:8 * y + 16], ctk, ["cf%d" % y])
    muk, cpk = ["mua", "mub"], ["cpa", "cpb"]
    act(T.ns8[:], T.cq[:].indirect(T.nbu[:]), ["cq", "nbu"], ["ns8"], 8.0)
    tt(T.ohw[:], T.cp[:].indirect(T.mu[:]), T.a0s[:], A.is_equal, cpk + muk + ["a0s"], ["ohw"])
    act(T.cpo[:], T.cp[:].indirect(T.pu[:]), cpk + puk, ["cpo"])
    for c in range(2):
        mm(2, 64 * c, 64, [(T.sgx[:, x, :], T.ohw[:, 64 * x:64 * x + 64], ["sgx%d" % x, "ohw"]) for x in range(2)])
    for j in range(8):
        out, sc = T.bd[:, :, 16 * j:16 * j + 16], T.gm[:, j:j + 1]
        if j < 5:
            ts(out, T.cfb[:], sc, None, A.mult, None, ["cf0", "cf1", "gm"], ["bd%d" % j])
        else:
            act(out, T.cfb[:], ["cf0", "cf1", "gm"], ["bd%d" % j], sc)
    bdk = ["bd%d" % j for j in range(8)]
    tt(T.ohz[:], T.cpo[:], bank(2)[:, 0:128], A.is_equal, ["cpo", "bank2"], ["ohz"])
    own("V", 0, 36, "win0c")

    def rows(b, oh, key):
        for y in range(2):
            out = bank(b)[:, y, :] if b == 3 else bank(b)[:, 64 * y:64 * y + 64]
            mmo(b, out, [(T.bd[:, 2 * x + y, :], oh[:, 64 * x:64 * x + 64], bdk + [key]) for x in range(2)])
    ev, od = T.ns8[:, 0::2], T.ns8[:, 1::2]

    def base(k):
        mm(4 + k, 0, 128, [(T.w3[:, 0, :], ev, ["w3l", "ns8"]), (T.w3[:, 1, :], od, ["w3h", "ns8"])], last=False)
    base(0)
    rows(3, T.ohz, "ohz")
    act(T.ms[:, 0:64], T.c48[:].indirect(T.mu[:, 0:4]), ["c48", "mua"], ["ms0"])
    act(T.ms[:, 64:128], T.c48[:].indirect(T.mu[:, 4:8]), ["c48", "mub", "c_big"], ["ms1"], bias=col("big"))
    own("S", 80, 96, "win0b")
    for n in range(2):
        act(T.rd[:, :, 64 * n:64 * n + 64], T.bank3[:, 0:2, :], ["bank3"], ["rd%d" % n])
    rdk = ["rd%d" % n for n in range(2)]
    own("S", 54, 80, "win0d")
    r1e, r1o, r2e, r2o = (T.rd[:, e, o::2] for e in range(2) for o in range(2))
    turn = [((low, r1e, "low"), (up, r1o, "up")), ((low, r2e, "low"), (high, r1o, "high")), ((down, r2e, "down"), (high, r2o, "high"))]
    base(1)
    base(2)
    for k in range(3):
        for n in range(2):
            mm(4 + k, 64 * n, 64, [(t, rh, [key] + rdk) for t, rh, key in turn[k]], first=False, last=n == 1)
    own("V", 36, 54, "win0e")
    mm(7, 0, 128, [(low, ev, ["low", "ns8"]), (high, od, ["high", "ns8"])])
    tt(T.oha[:], T.reln[:].indirect(T.pu[:]), T.ms[:], A.is_equal, relk + puk + ["ms0", "ms1"], ["oha"])
    rows(2, T.oha, "oha")
    for k in range(3):
        vcopy(T.lr0[:, 128 * k:128 * k + 128], bank(4 + k)[:, 0:128], ["bank%d" % (4 + k)], ["lr0%d" % k])

    def last1():
        act(T.ya[:], bank(2)[:, 0:128], ["bank2"], ["ya"])
        mmo(5, bank(5)[:, 0:96:3], [(same, T.ya[:, 0:64:2], ["same", "ya"])])
        middle(5, bank(5)[:, 1:96:3], (down, T.ya[:, 64:128:2], ["down", "ya"]), (up, T.ya[:, 1:64:2], ["up", "ya"]))
        mmo(5, bank(5)[:, 2:96:3], [(same, T.ya[:, 65:128:2], ["same", "ya"])])

    def last2():
        act(T.kb[:], bank(5)[:, 0:96], ["bank5"], ["kb"])
        for j in range(2):
            out, b, key = T["k%d" % (j + 1)], T.bcol[:, j:j + 1], "k%d" % (j + 1)
            op("S", lambda: s.activation(out[:], bank(5)[:, 0:96], SIGN, bias=b, scale=2.0), ["bank5", "bcol"], [key])
        mm(6, 0, 96, [(same, T.c8[:], ["same", "c8a", "c8b"]), (same, T.kb[:], ["kb"])] + [(T.id60[:], T[k][:], ["id60", k]) for k in ("k1", "k2")])

    hs = [slice(256 * h, 256 * h + 256) for h in range(2)]
    pb = {(0, 0): 0, (0, 1): 1, (0, 2): 2, (1, 0): 4, (1, 1): 5, (1, 2): 7}
    pcopy = {(1, 1, 0): 0, (1, 0, 0): 1}

    def win(t, k):
        return T.win0[:] if t == 0 else T.win1[:, 1024 * k:1024 * k + 1024]

    def lst(t, k, n, a=0, b=32):
        c = 128 * k + 32 * n if t == 0 else 32 * n
        return T.lr0[:, c + a:c + b] if t == 0 else T.lr1[:, c + a:c + b]

    def keys(t, k):
        return ["win0b", "win0c", "win0d", "win0e", "lr0%d" % k] if t == 0 else ["f1%d0" % k, "f1%d1" % k, "lr1"]

    def arrived(e, t, k):
        name = "arr0" if t == 0 else "arr1k%d" % k
        wait(e, name, narr[name])

    def buf(n, t, k):
        return T["%s%d%d" % (n, t, k)]

    def bk(n, t, k, h):
        return "%s%d%dh%d" % (n, t, k, h)

    def first(e, t, k, h, n=0):
        arrived(e, t, k)
        nm = "g" + "ab"[n]
        out, src, ky = buf(nm, t, k)[:, hs[h]], win(t, k).indirect(lst(t, k, n, 16 * h, 16 * h + 16)), keys(t, k)
        if e == "V":
            vcopy(out, src, ky, [bk(nm, t, k, h)])
        else:
            act(out, src, ky, [bk(nm, t, k, h)])

    def move(t, k, h):
        b = pcopy[t, k, h]
        act(bank(b)[:, hs[h]], buf("gb", t, k)[:, hs[h]], [bk("gb", t, k, h)], ["bank%d" % b])

    def gather(t, k, n, halves=(0, 1)):
        arrived("S", t, k)
        nm = "g" + "ab"[n]
        whole = t == 0 and k > 0 and len(halves) == 2
        if whole:
            act(buf(nm, t, k)[:], win(t, k).indirect(lst(t, k, n)), keys(t, k), [bk(nm, t, k, 0), bk(nm, t, k, 1)])
        for h in halves:
            if not whole:
                act(buf(nm, t, k)[:, hs[h]], win(t, k).indirect(lst(t, k, n, 16 * h, 16 * h + 16)), keys(t, k), [bk(nm, t, k, h)])
            if n == 1 and (t, k, h) in pcopy:
                move(t, k, h)
            elif n == 1:
                mm(pb[t, k], 256 * h, 256, [(T.idf[:], buf(nm, t, k)[:, hs[h]], ["idf", bk(nm, t, k, h)])])

    def result(k, h):
        return T.win1[:, 1024 * k + 256 * h:1024 * k + 256 * h + 256], "f1%d%d" % (k, h)

    def part(t, k, n, h):
        arrived("V", t, k)
        src, dst = {2: ("ga", "ma"), 3: ("ma", "mb"), 1: ("mb", "")}[n]
        out, key = result(k, h) if n == 1 else (buf(dst, t, k)[:, hs[h]], bk(dst, t, k, h))
        tt(out, win(t, k).indirect(lst(t, k, n, 16 * h, 16 * h + 16)), buf(src, t, k)[:, hs[h]], A.max, keys(t, k) + [bk(src, t, k, h)], [key])

    def join(k, h):
        out, key = result(k, h)
        b = pb[0, k]
        tt(out, bank(b)[:, hs[h]], buf("mb", 0, k)[:, hs[h]], A.max, ["bank%d" % b, bk("mb", 0, k, h)], [key])

    both, one = (0, 1), (1,)
    moved = {(0, 0): one, (0, 1): both, (0, 2): both, (1, 0): (1, 0), (1, 2): one}

    def block0(k):
        for n in (2, 3, 1):
            for h in range(2):
                if n == 1 and h in moved[0, k]:
                    join(k, h)
                else:
                    part(0, k, n, h)

    def slots1(k):
        w, ky = T.win1[:, 1024 * k:1024 * k + 512], ["f1%d0" % k, "f1%d1" % k, "ls1"]
        c1 = 1024 * k + 8 * (64 + 16 * r)
        out, srcs = T.win1[:, c1:c1 + 128], [T.snd1[:, k, 128 * j:128 * j + 128] for j in range(3)]
        if k < 2:
            act(srcs[2], w.indirect(T.ls1[:, 16:24]), ky, ["snd1%dr" % k])
            act(T.snd1[:, k, 0:256], w.indirect(T.ls1[:, 0:16]), ky, ["snd1%d" % k])
            relay(1 + k, srcs[2], ["snd1%dr" % k])
            fused(out, srcs, "arr1k%d" % k, ["snd1%d" % k])
        else:
            vcopy(T.lf[:], bank(6)[:, 0:96], ["bank6"], ["lf"])
            vcopy(srcs[2], w.indirect(T.ls1[:, 16:24]), ky, ["snd12c"])
            vcopy(T.snd1[:, k, 0:256], w.indirect(T.ls1[:, 0:16]), ky, ["snd12a"])
            single(out, srcs[2], "arr1k2", ["snd12c"])
            fused(out, srcs, "arr1k2", ["snd12a"])

    first("S", 0, 0, 0)
    first("V", 0, 0, 1)
    ts(T.ls1[:], bank(7)[:, 128:152], k8, None, A.add, None, ["bank7", "cf"], ["ls1"])
    ts(T.lr1[:], bank(7)[:, 0:128], k8, None, A.add, None, ["bank7", "cf"], ["lr1"])
    gather(0, 0, 1, moved[0, 0])
    gather(0, 1, 1, moved[0, 1])
    last1()
    gather(0, 1, 0)
    gather(0, 2, 1, (0,))
    block0(0)
    slots1(0)
    gather(0, 2, 0)
    gather(0, 2, 1, (1,))
    block0(1)
    slots1(1)
    last2()
    block0(2)
    first("S", 1, 0, 0)
    first("S", 1, 0, 1)
    slots1(2)
    gather(1, 0, 1, moved[1, 0])
    gather(1, 1, 0)
    first("S", 1, 1, 0, 1)
    gather(1, 1, 1, one)
    move(1, 1, 0)
    gather(1, 2, 0)
    gather(1, 2, 1, one)

    def join1(k, h):
        b = pcopy.get((1, k, h), pb[1, k])
        tt(T["n1h%d" % h][:, 256 * k:256 * k + 256], bank(b)[:, hs[h]], buf("mb", 1, k)[:, hs[h]], A.max,
           ["bank%d" % b, bk("mb", 1, k, h)], ["n1h%d%d" % (h, k)])

    def quarter(n, u):
        h, c = u // 2, slice(128 * u, 128 * u + 128)
        arrived("V", 1, 2)
        c2 = 512 + 128 * (u % 2)
        out, key = T["n1h%d" % h][:, c2:c2 + 128], "n1q%d" % u

        def mk(nm):
            return bk(nm, 1, 2, h) if nm[0] == "g" else "%sq%d" % (nm, u)
        if n == 1 and h in moved[1, 2]:
            b = pb[1, 2]
            tt(out, bank(b)[:, c], buf("mb", 1, 2)[:, c], A.max, ["bank%d" % b, mk("mb")], [key])
            return
        src, dst = {2: ("ga", "ma"), 3: ("ma", "mb"), 1: ("mb", "")}[n]
        if n != 1:
            out, key = buf(dst, 1, 2)[:, c], mk(dst)
        tt(out, win(1, 2).indirect(lst(1, 2, n, 8 * u, 8 * u + 8)), buf(src, 1, 2)[:, c], A.max, keys(1, 2) + [mk(src)], [key])

    def final(e, a, b):
        u = a // 24
        h, j = u // 2, u % 2
        out, src = T.yo[:, 16 * a:16 * b], T["n1h%d" % h][:, 128 * j:128 * j + 640].indirect(T.lf[:, a:b])
        ky = ["lf", "n1h%d0" % h, "n1h%d1" % h] + ["n1q%d" % w for w in range(2 * h, u + 1)]
        if e == "V":
            vcopy(out, src, ky, ["yo%d" % a])
        else:
            act(out, src, ky, ["yo%d" % a])

    def store(u, ks):
        op("Y", lambda: g.sync.dma_start(T.y[:, 384 * u:384 * u + 384], T.yo[:, 384 * u:384 * u + 384]), ["yo%d" % a for a in ks], [], "st%d" % u, 16)
    for k in range(2):
        for n in (2, 3):
            for h in range(2):
                part(1, k, n, h)
        join1(k, 0)
        if k == 0:
            join1(0, 1)
    for n, u in [(2, 0), (2, 1), (3, 0), (3, 1), (1, 0), (2, 2), (1, 1), (3, 2), (2, 3), (0, 1), (1, 2), (3, 3)]:
        if n == 0:
            join1(1, u)
        else:
            quarter(n, u)
    final("V", 48, 56)
    quarter(1, 3)
    final("S", 0, 24)
    store(0, [0])
    final("S", 24, 48)
    store(1, [24])
    final("S", 56, 72)
    store(2, [48, 56])
    final("V", 72, 84)
    final("S", 84, 96)
    store(3, [72, 84])
    for name in sorted(cnt):
        wait("Y", name, cnt[name])
    wait("G", "sent", nsent[0])
